import numpy as np
import ml_dtypes


def mxq(x, axis, fmt="e4m3"):
    dtype, down = {"e4m3": (ml_dtypes.float8_e4m3fn, 7), "e5m2": (ml_dtypes.float8_e5m2, 14)}[fmt]
    v = np.moveaxis(np.asarray(x, np.float32).astype(ml_dtypes.bfloat16).astype(np.float64), axis, -1)
    blocks = v.reshape(v.shape[:-1] + (-1, 32))
    amax = np.abs(blocks).max(-1, keepdims=True)
    byte = np.maximum(np.where(amax > 0, np.frexp(amax)[1] - 1 + 127, 0) - down, 1)
    scale = np.exp2(byte - 127.0)
    codes = (blocks / scale).astype(np.float32).astype(dtype).astype(np.float64)
    return np.moveaxis((codes * scale).reshape(v.shape), -1, axis)


WIDE = False


def mx_kscale(k):
    if not WIDE:
        return np.ones(k)
    levels = np.array([10, -10, 5, -5, 0])
    if k % 512:
        return np.exp2(np.random.permutation(np.resize(levels, k // 32))).repeat(32)
    a = np.empty((k // 512, 16))
    for p in range(k // 512):
        a[p, :8] = np.random.permutation(np.resize(levels, 8))
        for g in range(8):
            far = levels[np.abs(levels - a[p, g]) >= 10]
            a[p, g + 8] = far[np.random.randint(len(far))]
    return np.exp2(a.ravel()).repeat(32)


def f64(x):
    return np.asarray(x).astype(np.float64)


def striped(idx):
    return np.tile(idx.reshape(-1, 16).T, (8, 1)).astype(np.uint16)


def unstriped(offs):
    return offs[:16].T.reshape(-1).astype(np.int64)


def pack_weight(w):
    k, n = w.shape
    w = f64(np.asarray(w, np.float32).astype(ml_dtypes.bfloat16)).reshape(k // 32, 32, n)
    amax = np.abs(w).max(1)
    byte = np.clip(np.where(amax > 0, np.frexp(amax)[1] - 1 + 127 - 7, 1), 1, 254)
    scaled = (w * np.exp2(127.0 - byte)[:, None, :]).reshape(k, n).astype(np.float32)
    words = np.ascontiguousarray(scaled.reshape(k // 512, 128, 4, n).transpose(0, 1, 3, 2)).astype(ml_dtypes.float8_e4m3fn).view(np.uint8)
    return words, np.ascontiguousarray(byte.astype(np.uint8).reshape(k // 512, 16, n))


def unpack_weight(words, scales):
    g, p, n, _ = words.shape
    vals = np.ascontiguousarray(words).view(ml_dtypes.float8_e4m3fn).astype(np.float64) * np.repeat(np.exp2(scales.astype(np.float64) - 127.0), 8, axis=1)[..., None]
    return vals.transpose(0, 1, 3, 2).reshape(g * 512, n)


def planes(y):
    n, m = y.shape
    v = y.astype(np.float32).astype(ml_dtypes.bfloat16).astype(np.float64).reshape(n // 32, 32, m)
    top = np.abs(v).max(1)
    byte = np.clip(np.where(top > 0, np.frexp(top)[1] - 1 + 127 - 7, 1), 1, 254)
    codes = (v * np.exp2(127.0 - byte)[:, None, :]).reshape(n, m).astype(np.float32).astype(ml_dtypes.float8_e4m3fn).view(np.uint8)
    words = codes.reshape(n // 512, 128, 4, m).transpose(0, 1, 3, 2)
    return np.ascontiguousarray(words), np.ascontiguousarray(byte.astype(np.uint8).reshape(n // 512, 16, m))


def silu(v):
    return v / (1.0 + np.exp(-np.maximum(v, -700.0)))


K, T, S, J = 512, 2048, 512, 512


def setup_inputs():
    n = np.random.standard_normal
    s = mx_kscale(K)[:, None]
    packed_xT = pack_weight(n((K, T)) * s)
    packed_eT = pack_weight(n((K, T)) * s)
    return {
        "x_words": packed_xT[0],
        "x_scales": packed_xT[1],
        "e_words": packed_eT[0],
        "e_scales": packed_eT[1],
        "hT": (n((K, J)) / np.sqrt(K) / s).astype(np.float32),
        "offs": striped(np.random.permutation(T)[:S]),
    }


def reference(x_words, x_scales, e_words, e_scales, hT, offs):
    xq = unpack_weight(x_words, x_scales)[:, unstriped(offs)]
    hTq = mxq(f64(hT), 0, "e4m3")
    y = xq.T @ hTq
    e_offs = unpack_weight(e_words, e_scales)[:, unstriped(offs)]
    e = e_offs.T @ hTq
    out_0 = silu(y) * e
    return (out_0,) + planes(out_0)

@@ -1,0 +1,146 @@
+from contextlib import ExitStack
+
+import concourse.mybir as mybir
+
+F32 = mybir.dt.float32
+BF16 = mybir.dt.bfloat16
+I32 = mybir.dt.int32
+U32 = mybir.dt.uint32
+U16 = mybir.dt.uint16
+U8 = mybir.dt.uint8
+FP8X4 = mybir.dt.float8_e4m3fn_x4
+SILU = mybir.ActivationFunctionType.Silu
+MULT = mybir.AluOpType.mult
+
+P = 128
+PACK = 4
+K, T, S, J = 512, 2048, 512, 512
+CH = 128
+HALF = 256
+FLOPS = 2 * 2 * K * S * J
+
+
+def tile_picked_zdejag_silu_po_kernel(tc, x_words, x_scales, e_words, e_scales, hT, offs, out_0, out_1, out_2):
+    nc = tc.nc
+    with ExitStack() as ctx:
+        keep = ctx.enter_context(tc.tile_pool(name="keep", bufs=1))
+        psum = ctx.enter_context(tc.psum_pool(name="psum", bufs=1))
+
+        offsets = keep.tile([P, S // 16], U16, name="offsets")
+        nc.sync.dma_start(offsets[:], offs)
+
+        def load_scales(name, src, k, eng):
+            win = keep.tile([P, T], U8, name=name, align_bytes=64)
+            nc.vector.memset(win[:].bitcast(I32), 0)
+            for r in range(4):
+                eng.dma_start(win[k + r : P : 32, :].bitcast(I32), src[0, r:16:4, :].bitcast(I32))
+            return win
+
+        def load_words(name, src):
+            win = keep.tile([P, T], U32, name=name, align_bytes=64)
+            nc.sync.dma_start(win[:].bitcast(I32), src[0].rearrange("p n t -> p (n t)").bitcast(I32))
+            return win
+
+        def load_h(u):
+            raw = keep.tile([P, PACK, HALF], F32, name="hraw%d" % u)
+            nc.sync.dma_start(raw[:], hT.rearrange("(p t) j -> p t j", t=PACK)[:, :, u * HALF : (u + 1) * HALF])
+            return raw
+
+        xs_win = load_scales("xs_win", x_scales, 0, nc.scalar)
+        xw_win = load_words("xw_win", x_words)
+        es_win = load_scales("es_win", e_scales, 4, nc.gpsimd)
+        hraw = [load_h(0)]
+        ew_win = load_words("ew_win", e_words)
+        hraw.append(load_h(1))
+
+        warm = keep.tile([P, 8], F32, name="warm")
+        warm2 = keep.tile([P, 8], F32, name="warm2")
+        nc.vector.memset(warm[:], 0.0)
+        nc.scalar.activation(warm2[:], warm[:], SILU)
+
+        def gather_scales(name, win):
+            g = keep.tile([P, S], U8, name=name + "_g", align_bytes=64)
+            nc.vector.tensor_copy(g[:], win[:].indirect(offsets[:]))
+            return g
+
+        def deal_scales(name, g):
+            d = keep.tile([P, PACK, P], U8, name=name + "_d", align_bytes=64)
+            nc.vector.tensor_copy(d[:], g[:].rearrange("p (m t) -> p t m", t=PACK))
+            return d
+
+        def gather_words(name, win):
+            g = keep.tile([P, PACK, P], U32, name=name + "_g", align_bytes=64)
+            nc.vector.tensor_copy(g[:].rearrange("p t m -> p m t"), win[:].indirect(offsets[:]))
+            return g
+
+        xs_g = gather_scales("xs", xs_win)
+        es_g = gather_scales("es", es_win)
+        xs = deal_scales("xs", xs_g)
+        xw = gather_words("xw", xw_win)
+        es = deal_scales("es", es_g)
+
+        h_codes, h_scales = [], []
+
+        def quantise_h(u):
+            hb = keep.tile([P, HALF, PACK], BF16, name="hb%d" % u, align_bytes=64)
+            nc.scalar.copy(hb[:], hraw[u][:].rearrange("p t j -> p j t"))
+            c = keep.tile([P, HALF], U32, name="hc%d" % u, align_bytes=64)
+            s = keep.tile([P, HALF], U8, name="hs%d" % u, align_bytes=64)
+            nc.vector.quantize_mx(out=c[:].bitcast(FP8X4), scales=s[:], in_=hb[:].rearrange("p j t -> p (j t)"))
+            h_codes.append(c)
+            h_scales.append(s)
+
+        def product(name, words, scales, k, c):
+            bank = psum.tile([P, PACK, CH], F32, name="%s%d" % (name, c))
+            u, cols = c // 2, slice((c % 2) * CH, (c % 2 + 1) * CH)
+            for t in range(PACK):
+                nc.tensor.matmul_mx(out=bank[:, t, :], lhsT=words[:, t, :].bitcast(FP8X4), lhsT_scale=scales[k:P, t, :],
+                                    rhs=h_codes[u][:, cols].bitcast(FP8X4), rhs_scale=h_scales[u][:, cols], start=True, stop=True)
+            return bank
+
+        def gate(c):
+            y = product("y", xw, xs, 0, c)
+            g = keep.tile([P, PACK, CH], F32, name="gate%d" % c)
+            nc.scalar.activation(g[:], y[:], SILU)
+            return g
+
+        quantise_h(0)
+        gates = [gate(0), gate(1)]
+        ew = gather_words("ew", ew_win)
+        quantise_h(1)
+        gates.append(gate(2))
+        gates.append(gate(3))
+
+        o_codes = keep.tile([P, J], U32, name="o_codes", align_bytes=64)
+        o_scales = keep.tile([P, J], U8, name="o_scales", align_bytes=64)
+        out_rows = out_0.rearrange("(p t) j -> p t j", t=PACK)
+        out_words = out_1[0].rearrange("p n t -> p (n t)").bitcast(I32)
+        rounded = []
+
+        def combine(c):
+            e = product("e", ew, es, 4, c)
+            o = keep.tile([P, PACK, CH], F32, name="o%d" % c)
+            nc.vector.tensor_tensor(o[:], e[:], gates[c][:], MULT)
+            nc.sync.dma_start(out_rows[:, :, c * CH : (c + 1) * CH], o[:])
+            b = keep.tile([P, CH, PACK], BF16, name="ob%d" % c, align_bytes=64)
+            if c < 3:
+                nc.scalar.copy(b[:], o[:].rearrange("p t j -> p j t"))
+            else:
+                nc.vector.tensor_copy(b[:], o[:].rearrange("p t j -> p j t"))
+            rounded.append(b)
+
+        def quantise_out(c):
+            cols = slice(c * CH, (c + 1) * CH)
+            nc.vector.quantize_mx(out=o_codes[:, cols].bitcast(FP8X4), scales=o_scales[:, cols], in_=rounded[c][:].rearrange("p j t -> p (j t)"))
+            if c % 2 == 1:
+                half = slice((c - 1) * CH, (c + 1) * CH)
+                nc.sync.dma_start(out_words[:, half], o_codes[:, half].bitcast(I32))
+
+        combine(0)
+        for c in range(1, 4):
+            combine(c)
+            quantise_out(c - 1)
+        quantise_out(3)
+        for r in range(4):
+            eng = nc.scalar if r % 2 else nc.sync
+            eng.dma_start(out_2[0, r:16:4, :].bitcast(I32), o_scales[r:P:32, :].bitcast(I32))

@@ -16,7 +16,6 @@ P = 128
 PACK = 4
 K, T, S, J = 512, 2048, 512, 512
 CH = 128
-HALF = 256
 FLOPS = 2 * 2 * K * S * J
 
 
@@ -29,11 +28,11 @@ def tile_picked_zdejag_silu_po_kernel(tc, x_words, x_scales, e_words, e_scales, 
         offsets = keep.tile([P, S // 16], U16, name="offsets")
         nc.sync.dma_start(offsets[:], offs)
 
-        def load_scales(name, src, k, eng):
+        def load_scales(name, src, k, clear):
             win = keep.tile([P, T], U8, name=name, align_bytes=64)
-            nc.vector.memset(win[:].bitcast(I32), 0)
+            clear.memset(win[:].bitcast(I32), 0)
             for r in range(4):
-                eng.dma_start(win[k + r : P : 32, :].bitcast(I32), src[0, r:16:4, :].bitcast(I32))
+                nc.sync.dma_start(win[k + r : P : 32, :].bitcast(I32), src[0, r:16:4, :].bitcast(I32))
             return win
 
         def load_words(name, src):
@@ -41,17 +40,22 @@ def tile_picked_zdejag_silu_po_kernel(tc, x_words, x_scales, e_words, e_scales, 
             nc.sync.dma_start(win[:].bitcast(I32), src[0].rearrange("p n t -> p (n t)").bitcast(I32))
             return win
 
-        def load_h(u):
-            raw = keep.tile([P, PACK, HALF], F32, name="hraw%d" % u)
-            nc.sync.dma_start(raw[:], hT.rearrange("(p t) j -> p t j", t=PACK)[:, :, u * HALF : (u + 1) * HALF])
+        def load_h(c0, c1, parts=1):
+            raw = keep.tile([P, PACK, (c1 - c0) * CH], F32, name="hraw%d" % c0)
+            for i in range(parts):
+                rows = slice(i * PACK // parts, (i + 1) * PACK // parts)
+                nc.sync.dma_start(raw[:, rows, :], hT.rearrange("(p t) j -> p t j", t=PACK)[:, rows, c0 * CH : c1 * CH])
             return raw
 
-        xs_win = load_scales("xs_win", x_scales, 0, nc.scalar)
+        def interleave(copy, dst, src):
+            copy(dst.rearrange("p (c i) t -> p c t i", i=4), src.rearrange("p t (c i) -> p c t i", i=4))
+
+        h_a = load_h(0, 1, 2)
+        xs_win = load_scales("xs_win", x_scales, 0, nc.vector)
+        h_b = load_h(1, 4)
         xw_win = load_words("xw_win", x_words)
         es_win = load_scales("es_win", e_scales, 4, nc.gpsimd)
-        hraw = [load_h(0)]
         ew_win = load_words("ew_win", e_words)
-        hraw.append(load_h(1))
 
         warm = keep.tile([P, 8], F32, name="warm")
         warm2 = keep.tile([P, 8], F32, name="warm2")
@@ -73,29 +77,24 @@ def tile_picked_zdejag_silu_po_kernel(tc, x_words, x_scales, e_words, e_scales, 
             nc.vector.tensor_copy(g[:].rearrange("p t m -> p m t"), win[:].indirect(offsets[:]))
             return g
 
-        xs_g = gather_scales("xs", xs_win)
-        es_g = gather_scales("es", es_win)
-        xs = deal_scales("xs", xs_g)
-        xw = gather_words("xw", xw_win)
-        es = deal_scales("es", es_g)
-
         h_codes, h_scales = [], []
 
-        def quantise_h(u):
-            hb = keep.tile([P, HALF, PACK], BF16, name="hb%d" % u, align_bytes=64)
-            nc.scalar.copy(hb[:], hraw[u][:].rearrange("p t j -> p j t"))
-            c = keep.tile([P, HALF], U32, name="hc%d" % u, align_bytes=64)
-            s = keep.tile([P, HALF], U8, name="hs%d" % u, align_bytes=64)
+        def quantise_h(name, raw, chunks):
+            w = chunks * CH
+            hb = keep.tile([P, w, PACK], BF16, name="hb" + name, align_bytes=64)
+            interleave(nc.scalar.copy, hb[:], raw)
+            c = keep.tile([P, w], U32, name="hc" + name, align_bytes=64)
+            s = keep.tile([P, w], U8, name="hs" + name, align_bytes=64)
             nc.vector.quantize_mx(out=c[:].bitcast(FP8X4), scales=s[:], in_=hb[:].rearrange("p j t -> p (j t)"))
-            h_codes.append(c)
-            h_scales.append(s)
+            for i in range(chunks):
+                h_codes.append(c[:, i * CH : (i + 1) * CH])
+                h_scales.append(s[:, i * CH : (i + 1) * CH])
 
         def product(name, words, scales, k, c):
             bank = psum.tile([P, PACK, CH], F32, name="%s%d" % (name, c))
-            u, cols = c // 2, slice((c % 2) * CH, (c % 2 + 1) * CH)
             for t in range(PACK):
                 nc.tensor.matmul_mx(out=bank[:, t, :], lhsT=words[:, t, :].bitcast(FP8X4), lhsT_scale=scales[k:P, t, :],
-                                    rhs=h_codes[u][:, cols].bitcast(FP8X4), rhs_scale=h_scales[u][:, cols], start=True, stop=True)
+                                    rhs=h_codes[c].bitcast(FP8X4), rhs_scale=h_scales[c], start=True, stop=True)
             return bank
 
         def gate(c):
@@ -104,12 +103,16 @@ def tile_picked_zdejag_silu_po_kernel(tc, x_words, x_scales, e_words, e_scales, 
             nc.scalar.activation(g[:], y[:], SILU)
             return g
 
-        quantise_h(0)
-        gates = [gate(0), gate(1)]
+        xs_g = gather_scales("xs", xs_win)
+        quantise_h("a", h_a[:], 1)
+        xs = deal_scales("xs", xs_g)
+        quantise_h("b", h_b[:, :, 0:CH], 1)
+        quantise_h("c", h_b[:, :, CH : 3 * CH], 2)
+        xw = gather_words("xw", xw_win)
+        es_g = gather_scales("es", es_win)
+        gates = [gate(0), gate(1), gate(2), gate(3)]
+        es = deal_scales("es", es_g)
         ew = gather_words("ew", ew_win)
-        quantise_h(1)
-        gates.append(gate(2))
-        gates.append(gate(3))
 
         o_codes = keep.tile([P, J], U32, name="o_codes", align_bytes=64)
         o_scales = keep.tile([P, J], U8, name="o_scales", align_bytes=64)
@@ -123,18 +126,15 @@ def tile_picked_zdejag_silu_po_kernel(tc, x_words, x_scales, e_words, e_scales, 
             nc.vector.tensor_tensor(o[:], e[:], gates[c][:], MULT)
             nc.sync.dma_start(out_rows[:, :, c * CH : (c + 1) * CH], o[:])
             b = keep.tile([P, CH, PACK], BF16, name="ob%d" % c, align_bytes=64)
-            if c < 3:
-                nc.scalar.copy(b[:], o[:].rearrange("p t j -> p j t"))
-            else:
-                nc.vector.tensor_copy(b[:], o[:].rearrange("p t j -> p j t"))
+            interleave(nc.scalar.copy if c < 3 else nc.vector.tensor_copy, b[:], o[:])
             rounded.append(b)
 
         def quantise_out(c):
             cols = slice(c * CH, (c + 1) * CH)
             nc.vector.quantize_mx(out=o_codes[:, cols].bitcast(FP8X4), scales=o_scales[:, cols], in_=rounded[c][:].rearrange("p j t -> p (j t)"))
-            if c % 2 == 1:
-                half = slice((c - 1) * CH, (c + 1) * CH)
-                nc.sync.dma_start(out_words[:, half], o_codes[:, half].bitcast(I32))
+            if c >= 2:
+                part = slice(0, 3 * CH) if c == 2 else cols
+                nc.sync.dma_start(out_words[:, part], o_codes[:, part].bitcast(I32))
 
         combine(0)
         for c in range(1, 4):
@@ -142,5 +142,5 @@ def tile_picked_zdejag_silu_po_kernel(tc, x_words, x_scales, e_words, e_scales, 
             quantise_out(c - 1)
         quantise_out(3)
         for r in range(4):
-            eng = nc.scalar if r % 2 else nc.sync
+            eng = nc.scalar if r % 2 == 0 else nc.sync
             eng.dma_start(out_2[0, r:16:4, :].bitcast(I32), o_scales[r:P:32, :].bitcast(I32))

@@ -16,6 +16,7 @@ P = 128
 PACK = 4
 K, T, S, J = 512, 2048, 512, 512
 CH = 128
+HALF = 256
 FLOPS = 2 * 2 * K * S * J
 
 
@@ -77,40 +78,37 @@ def tile_picked_zdejag_silu_po_kernel(tc, x_words, x_scales, e_words, e_scales, 
             nc.vector.tensor_copy(g[:].rearrange("p t m -> p m t"), win[:].indirect(offsets[:]))
             return g
 
-        h_codes, h_scales = [], []
+        h_codes = keep.tile([P, J], U32, name="h_codes", align_bytes=64)
+        h_scales = keep.tile([P, J], U8, name="h_scales", align_bytes=64)
 
-        def quantise_h(name, raw, chunks):
-            w = chunks * CH
-            hb = keep.tile([P, w, PACK], BF16, name="hb" + name, align_bytes=64)
+        def quantise_h(raw, j0, j1):
+            hb = keep.tile([P, j1 - j0, PACK], BF16, name="hb%d" % j0, align_bytes=64)
             interleave(nc.scalar.copy, hb[:], raw)
-            c = keep.tile([P, w], U32, name="hc" + name, align_bytes=64)
-            s = keep.tile([P, w], U8, name="hs" + name, align_bytes=64)
-            nc.vector.quantize_mx(out=c[:].bitcast(FP8X4), scales=s[:], in_=hb[:].rearrange("p j t -> p (j t)"))
-            for i in range(chunks):
-                h_codes.append(c[:, i * CH : (i + 1) * CH])
-                h_scales.append(s[:, i * CH : (i + 1) * CH])
+            nc.vector.quantize_mx(out=h_codes[:, j0:j1].bitcast(FP8X4), scales=h_scales[:, j0:j1], in_=hb[:].rearrange("p j t -> p (j t)"))
 
-        def product(name, words, scales, k, c):
-            bank = psum.tile([P, PACK, CH], F32, name="%s%d" % (name, c))
-            for t in range(PACK):
-                nc.tensor.matmul_mx(out=bank[:, t, :], lhsT=words[:, t, :].bitcast(FP8X4), lhsT_scale=scales[k:P, t, :],
-                                    rhs=h_codes[c].bitcast(FP8X4), rhs_scale=h_scales[c], start=True, stop=True)
+        def product(name, words, scales, k, u, v):
+            bank = psum.tile([P, 2, HALF], F32, name="%s%d%d" % (name, u, v))
+            cols = slice(u * HALF, (u + 1) * HALF)
+            for i in range(2):
+                t = 2 * v + i
+                nc.tensor.matmul_mx(out=bank[:, i, :], lhsT=words[:, t, :].bitcast(FP8X4), lhsT_scale=scales[k:P, t, :],
+                                    rhs=h_codes[:, cols].bitcast(FP8X4), rhs_scale=h_scales[:, cols], start=True, stop=True)
             return bank
 
-        def gate(c):
-            y = product("y", xw, xs, 0, c)
-            g = keep.tile([P, PACK, CH], F32, name="gate%d" % c)
+        def gate(u, v):
+            y = product("y", xw, xs, 0, u, v)
+            g = keep.tile([P, 2, HALF], F32, name="gate%d%d" % (u, v))
             nc.scalar.activation(g[:], y[:], SILU)
             return g
 
         xs_g = gather_scales("xs", xs_win)
-        quantise_h("a", h_a[:], 1)
+        quantise_h(h_a[:], 0, CH)
         xs = deal_scales("xs", xs_g)
-        quantise_h("b", h_b[:, :, 0:CH], 1)
-        quantise_h("c", h_b[:, :, CH : 3 * CH], 2)
+        quantise_h(h_b[:, :, 0:CH], CH, 2 * CH)
+        quantise_h(h_b[:, :, CH : 3 * CH], 2 * CH, 4 * CH)
         xw = gather_words("xw", xw_win)
         es_g = gather_scales("es", es_win)
-        gates = [gate(0), gate(1), gate(2), gate(3)]
+        gates = [[gate(u, v) for v in range(2)] for u in range(2)]
         es = deal_scales("es", es_g)
         ew = gather_words("ew", ew_win)
 
@@ -120,27 +118,21 @@ def tile_picked_zdejag_silu_po_kernel(tc, x_words, x_scales, e_words, e_scales, 
         out_words = out_1[0].rearrange("p n t -> p (n t)").bitcast(I32)
         rounded = []
 
-        def combine(c):
-            e = product("e", ew, es, 4, c)
-            o = keep.tile([P, PACK, CH], F32, name="o%d" % c)
-            nc.vector.tensor_tensor(o[:], e[:], gates[c][:], MULT)
-            nc.sync.dma_start(out_rows[:, :, c * CH : (c + 1) * CH], o[:])
-            b = keep.tile([P, CH, PACK], BF16, name="ob%d" % c, align_bytes=64)
-            interleave(nc.scalar.copy if c < 3 else nc.vector.tensor_copy, b[:], o[:])
+        for u in range(2):
+            cols = slice(u * HALF, (u + 1) * HALF)
+            o = keep.tile([P, PACK, HALF], F32, name="o%d" % u)
+            for v in range(2):
+                e = product("e", ew, es, 4, u, v)
+                rows = slice(2 * v, 2 * v + 2)
+                nc.vector.tensor_tensor(o[:, rows, :], e[:], gates[u][v][:], MULT)
+                nc.sync.dma_start(out_rows[:, rows, cols], o[:, rows, :])
+            b = keep.tile([P, HALF, PACK], BF16, name="ob%d" % u, align_bytes=64)
+            interleave(nc.scalar.copy if u == 0 else nc.vector.tensor_copy, b[:], o[:])
             rounded.append(b)
-
-        def quantise_out(c):
-            cols = slice(c * CH, (c + 1) * CH)
-            nc.vector.quantize_mx(out=o_codes[:, cols].bitcast(FP8X4), scales=o_scales[:, cols], in_=rounded[c][:].rearrange("p j t -> p (j t)"))
-            if c >= 2:
-                part = slice(0, 3 * CH) if c == 2 else cols
-                nc.sync.dma_start(out_words[:, part], o_codes[:, part].bitcast(I32))
-
-        combine(0)
-        for c in range(1, 4):
-            combine(c)
-            quantise_out(c - 1)
-        quantise_out(3)
+        for u in range(2):
+            cols = slice(u * HALF, (u + 1) * HALF)
+            nc.vector.quantize_mx(out=o_codes[:, cols].bitcast(FP8X4), scales=o_scales[:, cols], in_=rounded[u][:].rearrange("p j t -> p (j t)"))
+            nc.sync.dma_start(out_words[:, cols], o_codes[:, cols].bitcast(I32))
         for r in range(4):
             eng = nc.scalar if r % 2 == 0 else nc.sync
             eng.dma_start(out_2[0, r:16:4, :].bitcast(I32), o_scales[r:P:32, :].bitcast(I32))

@@ -51,9 +51,9 @@ def tile_picked_zdejag_silu_po_kernel(tc, x_words, x_scales, e_words, e_scales, 
         def interleave(copy, dst, src):
             copy(dst.rearrange("p (c i) t -> p c t i", i=4), src.rearrange("p t (c i) -> p c t i", i=4))
 
-        h_a = load_h(0, 1, 2)
+        h_a = load_h(0, 2, 2)
         xs_win = load_scales("xs_win", x_scales, 0, nc.vector)
-        h_b = load_h(1, 4)
+        h_b = load_h(2, 4)
         xw_win = load_words("xw_win", x_words)
         es_win = load_scales("es_win", e_scales, 4, nc.gpsimd)
         ew_win = load_words("ew_win", e_words)
@@ -102,10 +102,9 @@ def tile_picked_zdejag_silu_po_kernel(tc, x_words, x_scales, e_words, e_scales, 
             return g
 
         xs_g = gather_scales("xs", xs_win)
-        quantise_h(h_a[:], 0, CH)
+        quantise_h(h_a[:], 0, HALF)
         xs = deal_scales("xs", xs_g)
-        quantise_h(h_b[:, :, 0:CH], CH, 2 * CH)
-        quantise_h(h_b[:, :, CH : 3 * CH], 2 * CH, 4 * CH)
+        quantise_h(h_b[:], HALF, J)
         xw = gather_words("xw", xw_win)
         es_g = gather_scales("es", es_win)
         gates = [[gate(u, v) for v in range(2)] for u in range(2)]
@@ -127,7 +126,10 @@ def tile_picked_zdejag_silu_po_kernel(tc, x_words, x_scales, e_words, e_scales, 
                 nc.vector.tensor_tensor(o[:, rows, :], e[:], gates[u][v][:], MULT)
                 nc.sync.dma_start(out_rows[:, rows, cols], o[:, rows, :])
             b = keep.tile([P, HALF, PACK], BF16, name="ob%d" % u, align_bytes=64)
-            interleave(nc.scalar.copy if u == 0 else nc.vector.tensor_copy, b[:], o[:])
+            split = HALF if u == 0 else 96
+            interleave(nc.scalar.copy, b[:, 0:split, :], o[:, :, 0:split])
+            if split < HALF:
+                interleave(nc.vector.tensor_copy, b[:, split:HALF, :], o[:, :, split:HALF])
             rounded.append(b)
         for u in range(2):
             cols = slice(u * HALF, (u + 1) * HALF)

@@ -15,7 +15,6 @@ MULT = mybir.AluOpType.mult
 P = 128
 PACK = 4
 K, T, S, J = 512, 2048, 512, 512
-CH = 128
 HALF = 256
 FLOPS = 2 * 2 * K * S * J
 
@@ -30,7 +29,7 @@ def tile_picked_zdejag_silu_po_kernel(tc, x_words, x_scales, e_words, e_scales, 
         nc.sync.dma_start(offsets[:], offs)
 
         def load_scales(name, src, k, clear):
-            win = keep.tile([P, T], U8, name=name, align_bytes=64)
+            win = keep.tile([P, T], U8, name=name, tag=name, align_bytes=64)
             clear.memset(win[:].bitcast(I32), 0)
             for r in range(4):
                 nc.sync.dma_start(win[k + r : P : 32, :].bitcast(I32), src[0, r:16:4, :].bitcast(I32))
@@ -41,21 +40,20 @@ def tile_picked_zdejag_silu_po_kernel(tc, x_words, x_scales, e_words, e_scales, 
             nc.sync.dma_start(win[:].bitcast(I32), src[0].rearrange("p n t -> p (n t)").bitcast(I32))
             return win
 
-        def load_h(c0, c1, parts=1):
-            raw = keep.tile([P, PACK, (c1 - c0) * CH], F32, name="hraw%d" % c0)
-            for i in range(parts):
-                rows = slice(i * PACK // parts, (i + 1) * PACK // parts)
-                nc.sync.dma_start(raw[:, rows, :], hT.rearrange("(p t) j -> p t j", t=PACK)[:, rows, c0 * CH : c1 * CH])
-            return raw
+        def load_h(raw, u, t0, t1):
+            nc.sync.dma_start(raw[:, t0:t1, :], hT.rearrange("(p t) j -> p t j", t=PACK)[:, t0:t1, u * HALF : (u + 1) * HALF])
 
         def interleave(copy, dst, src):
             copy(dst.rearrange("p (c i) t -> p c t i", i=4), src.rearrange("p t (c i) -> p c t i", i=4))
 
-        h_a = load_h(0, 2, 2)
+        h_a = keep.tile([P, PACK, HALF], F32, name="h_a")
+        h_b = keep.tile([P, PACK, HALF], F32, name="h_b", tag="gate0")
+        load_h(h_a, 0, 0, 2)
+        load_h(h_a, 0, 2, 4)
         xs_win = load_scales("xs_win", x_scales, 0, nc.vector)
-        h_b = load_h(2, 4)
         xw_win = load_words("xw_win", x_words)
         es_win = load_scales("es_win", e_scales, 4, nc.gpsimd)
+        load_h(h_b, 1, 0, 4)
         ew_win = load_words("ew_win", e_words)
 
         warm = keep.tile([P, 8], F32, name="warm")
@@ -73,43 +71,48 @@ def tile_picked_zdejag_silu_po_kernel(tc, x_words, x_scales, e_words, e_scales, 
             nc.vector.tensor_copy(d[:], g[:].rearrange("p (m t) -> p t m", t=PACK))
             return d
 
-        def gather_words(name, win):
-            g = keep.tile([P, PACK, P], U32, name=name + "_g", align_bytes=64)
+        def gather_words(name, win, tag):
+            g = keep.tile([P, PACK, P], U32, name=name + "_g", tag=tag, align_bytes=64)
             nc.vector.tensor_copy(g[:].rearrange("p t m -> p m t"), win[:].indirect(offsets[:]))
             return g
 
-        h_codes = keep.tile([P, J], U32, name="h_codes", align_bytes=64)
-        h_scales = keep.tile([P, J], U8, name="h_scales", align_bytes=64)
+        h_codes = []
+        h_scales = []
 
-        def quantise_h(raw, j0, j1):
-            hb = keep.tile([P, j1 - j0, PACK], BF16, name="hb%d" % j0, align_bytes=64)
+        def quantise_h(raw, u, tag):
+            hb = keep.tile([P, HALF, PACK], BF16, name="hb%d" % u, tag="hb%d" % u, align_bytes=64)
             interleave(nc.scalar.copy, hb[:], raw)
-            nc.vector.quantize_mx(out=h_codes[:, j0:j1].bitcast(FP8X4), scales=h_scales[:, j0:j1], in_=hb[:].rearrange("p j t -> p (j t)"))
+            codes = keep.tile([P, HALF], U32, name="h_codes%d" % u, tag=tag, align_bytes=64)
+            scales = keep.tile([P, HALF], U8, name="h_scales%d" % u, align_bytes=64)
+            nc.vector.quantize_mx(out=codes[:].bitcast(FP8X4), scales=scales[:], in_=hb[:].rearrange("p j t -> p (j t)"))
+            h_codes.append(codes)
+            h_scales.append(scales)
 
         def product(name, words, scales, k, u, v):
             bank = psum.tile([P, 2, HALF], F32, name="%s%d%d" % (name, u, v))
-            cols = slice(u * HALF, (u + 1) * HALF)
             for i in range(2):
                 t = 2 * v + i
                 nc.tensor.matmul_mx(out=bank[:, i, :], lhsT=words[:, t, :].bitcast(FP8X4), lhsT_scale=scales[k:P, t, :],
-                                    rhs=h_codes[:, cols].bitcast(FP8X4), rhs_scale=h_scales[:, cols], start=True, stop=True)
+                                    rhs=h_codes[u][:].bitcast(FP8X4), rhs_scale=h_scales[u][:], start=True, stop=True)
             return bank
 
-        def gate(u, v):
-            y = product("y", xw, xs, 0, u, v)
-            g = keep.tile([P, 2, HALF], F32, name="gate%d%d" % (u, v))
-            nc.scalar.activation(g[:], y[:], SILU)
+        def gate(y, u):
+            g = keep.tile([P, PACK, HALF], F32, name="gate%d" % u, tag="gate%d" % u)
+            for v in range(2):
+                nc.scalar.activation(g[:, 2 * v : 2 * v + 2, :], y[v][:], SILU)
             return g
 
         xs_g = gather_scales("xs", xs_win)
-        quantise_h(h_a[:], 0, HALF)
+        quantise_h(h_a[:], 0, "xs_win")
         xs = deal_scales("xs", xs_g)
-        quantise_h(h_b[:], HALF, J)
-        xw = gather_words("xw", xw_win)
+        xw = gather_words("xw", xw_win, "xw_g")
+        ys = [[product("y", xw, xs, 0, 0, v) for v in range(2)]]
         es_g = gather_scales("es", es_win)
-        gates = [[gate(u, v) for v in range(2)] for u in range(2)]
         es = deal_scales("es", es_g)
-        ew = gather_words("ew", ew_win)
+        quantise_h(h_b[:], 1, "h_codes1")
+        ys.append([product("y", xw, xs, 0, 1, v) for v in range(2)])
+        gates = [gate(ys[u], u) for u in range(2)]
+        ew = gather_words("ew", ew_win, "hb1")
 
         o_codes = keep.tile([P, J], U32, name="o_codes", align_bytes=64)
         o_scales = keep.tile([P, J], U8, name="o_scales", align_bytes=64)
@@ -123,7 +126,7 @@ def tile_picked_zdejag_silu_po_kernel(tc, x_words, x_scales, e_words, e_scales, 
             for v in range(2):
                 e = product("e", ew, es, 4, u, v)
                 rows = slice(2 * v, 2 * v + 2)
-                nc.vector.tensor_tensor(o[:, rows, :], e[:], gates[u][v][:], MULT)
+                nc.vector.tensor_tensor(o[:, rows, :], e[:], gates[u][:, rows, :], MULT)
                 nc.sync.dma_start(out_rows[:, rows, cols], o[:, rows, :])
             b = keep.tile([P, HALF, PACK], BF16, name="ob%d" % u, align_bytes=64)
             split = HALF if u == 0 else 96

@@ -48,8 +48,7 @@ def tile_picked_zdejag_silu_po_kernel(tc, x_words, x_scales, e_words, e_scales, 
 
         h_a = keep.tile([P, PACK, HALF], F32, name="h_a")
         h_b = keep.tile([P, PACK, HALF], F32, name="h_b", tag="gate0")
-        load_h(h_a, 0, 0, 2)
-        load_h(h_a, 0, 2, 4)
+        load_h(h_a, 0, 0, 4)
         xs_win = load_scales("xs_win", x_scales, 0, nc.vector)
         xw_win = load_words("xw_win", x_words)
         es_win = load_scales("es_win", e_scales, 4, nc.gpsimd)
@@ -89,7 +88,7 @@ def tile_picked_zdejag_silu_po_kernel(tc, x_words, x_scales, e_words, e_scales, 
             h_scales.append(scales)
 
         def product(name, words, scales, k, u, v):
-            bank = psum.tile([P, 2, HALF], F32, name="%s%d%d" % (name, u, v))
+            bank = psum.tile([P, 2, HALF], F32, name="%s%d%d" % (name, u, v), tag="%s%d%d" % (name, u, v))
             for i in range(2):
                 t = 2 * v + i
                 nc.tensor.matmul_mx(out=bank[:, i, :], lhsT=words[:, t, :].bitcast(FP8X4), lhsT_scale=scales[k:P, t, :],
@@ -120,19 +119,40 @@ def tile_picked_zdejag_silu_po_kernel(tc, x_words, x_scales, e_words, e_scales, 
         out_words = out_1[0].rearrange("p n t -> p (n t)").bitcast(I32)
         rounded = []
 
-        for u in range(2):
-            cols = slice(u * HALF, (u + 1) * HALF)
-            o = keep.tile([P, PACK, HALF], F32, name="o%d" % u)
-            for v in range(2):
-                e = product("e", ew, es, 4, u, v)
-                rows = slice(2 * v, 2 * v + 2)
-                nc.vector.tensor_tensor(o[:, rows, :], e[:], gates[u][:, rows, :], MULT)
-                nc.sync.dma_start(out_rows[:, rows, cols], o[:, rows, :])
+        o = [keep.tile([P, PACK, HALF], F32, name="o%d" % u) for u in range(2)]
+
+        def store(u, v):
+            nc.sync.dma_start(out_rows[:, 2 * v : 2 * v + 2, u * HALF : (u + 1) * HALF], o[u][:, 2 * v : 2 * v + 2, :])
+
+        def multiply(u, v):
+            e = product("e", ew, es, 4, u, v)
+            rows = slice(2 * v, 2 * v + 2)
+            nc.vector.tensor_tensor(o[u][:, rows, :], e[:], gates[u][:, rows, :], MULT)
+            store(u, v)
+
+        def one_plane(name, u, t):
+            bank = psum.tile([P, HALF], F32, name=name, tag=name)
+            nc.tensor.matmul_mx(out=bank[:], lhsT=ew[:, t, :].bitcast(FP8X4), lhsT_scale=es[4:P, t, :],
+                                rhs=h_codes[u][:].bitcast(FP8X4), rhs_scale=h_scales[u][:], start=True, stop=True)
+            return bank
+
+        for t in range(2):
+            e_first = one_plane("e_first%d" % t, 0, t)
+            nc.vector.tensor_tensor(o[0][:, t, :], e_first[:], gates[0][:, t, :], MULT)
+            nc.sync.dma_start(out_rows[:, t, 0:HALF], o[0][:, t, :])
+        e_side = one_plane("y01", 1, 3)
+        e_sbuf = keep.tile([P, HALF], F32, name="e_sbuf")
+        nc.scalar.copy(e_sbuf[:], e_side[:])
+        nc.gpsimd.tensor_tensor(o[1][:, 3, :], e_sbuf[:], gates[1][:, 3, :], MULT)
+        multiply(0, 1)
+        multiply(1, 0)
+        e_last = one_plane("y00", 1, 2)
+        nc.vector.tensor_tensor(o[1][:, 2, :], e_last[:], gates[1][:, 2, :], MULT)
+        store(1, 1)
+        for u, split in enumerate((192, 80)):
             b = keep.tile([P, HALF, PACK], BF16, name="ob%d" % u, align_bytes=64)
-            split = HALF if u == 0 else 96
-            interleave(nc.scalar.copy, b[:, 0:split, :], o[:, :, 0:split])
-            if split < HALF:
-                interleave(nc.vector.tensor_copy, b[:, split:HALF, :], o[:, :, split:HALF])
+            interleave(nc.scalar.copy, b[:, 0:split, :], o[u][:, :, 0:split])
+            interleave(nc.vector.tensor_copy, b[:, split:HALF, :], o[u][:, :, split:HALF])
             rounded.append(b)
         for u in range(2):
             cols = slice(u * HALF, (u + 1) * HALF)

@@ -23,36 +23,32 @@ def tile_picked_zdejag_silu_po_kernel(tc, x_words, x_scales, e_words, e_scales, 
     nc = tc.nc
     with ExitStack() as ctx:
         keep = ctx.enter_context(tc.tile_pool(name="keep", bufs=1))
+        laid = ctx.enter_context(tc.tile_pool(name="laid", bufs=1))
         psum = ctx.enter_context(tc.psum_pool(name="psum", bufs=1))
 
         offsets = keep.tile([P, S // 16], U16, name="offsets")
         nc.sync.dma_start(offsets[:], offs)
 
-        def load_scales(name, src, k, clear):
-            win = keep.tile([P, T], U8, name=name, tag=name, align_bytes=64)
-            clear.memset(win[:].bitcast(I32), 0)
-            for r in range(4):
-                nc.sync.dma_start(win[k + r : P : 32, :].bitcast(I32), src[0, r:16:4, :].bitcast(I32))
-            return win
-
         def load_words(name, src):
-            win = keep.tile([P, T], U32, name=name, align_bytes=64)
+            win = keep.tile([P, T], U32, name=name, tag=name, align_bytes=64)
             nc.sync.dma_start(win[:].bitcast(I32), src[0].rearrange("p n t -> p (n t)").bitcast(I32))
             return win
-
-        def load_h(raw, u, t0, t1):
-            nc.sync.dma_start(raw[:, t0:t1, :], hT.rearrange("(p t) j -> p t j", t=PACK)[:, t0:t1, u * HALF : (u + 1) * HALF])
 
         def interleave(copy, dst, src):
             copy(dst.rearrange("p (c i) t -> p c t i", i=4), src.rearrange("p t (c i) -> p c t i", i=4))
 
-        h_a = keep.tile([P, PACK, HALF], F32, name="h_a")
-        h_b = keep.tile([P, PACK, HALF], F32, name="h_b", tag="gate0")
-        load_h(h_a, 0, 0, 4)
-        xs_win = load_scales("xs_win", x_scales, 0, nc.vector)
+        h_rows = hT.rearrange("(p t) j -> p t j", t=PACK)
+        h_raw = keep.tile([P, PACK, J], F32, name="h_raw", tag="gates")
+        nc.sync.dma_start(h_raw[:, 0:2, :], h_rows[:, 0:2, :])
+        xs_win = laid.tile([P, T], U8, name="xs_win", align_bytes=64, offset=0)
+        nc.vector.memset(xs_win[:].bitcast(I32), 0)
+        for r in range(4):
+            nc.sync.dma_start(xs_win[r:P:32, :].bitcast(I32), x_scales[0, r:16:4, :].bitcast(I32))
+        es_win = laid.tile([P, T], U8, name="es_win", align_bytes=64, offset=T)
+        nc.gpsimd.memset(es_win[:].bitcast(I32), 0)
+        nc.sync.dma_start(es_win[4:P:8, :].bitcast(I32), e_scales[0].bitcast(I32))
+        nc.sync.dma_start(h_raw[:, 2:4, :], h_rows[:, 2:4, :])
         xw_win = load_words("xw_win", x_words)
-        es_win = load_scales("es_win", e_scales, 4, nc.gpsimd)
-        load_h(h_b, 1, 0, 4)
         ew_win = load_words("ew_win", e_words)
 
         warm = keep.tile([P, 8], F32, name="warm")
@@ -65,9 +61,8 @@ def tile_picked_zdejag_silu_po_kernel(tc, x_words, x_scales, e_words, e_scales, 
             nc.vector.tensor_copy(g[:], win[:].indirect(offsets[:]))
             return g
 
-        def deal_scales(name, g):
-            d = keep.tile([P, PACK, P], U8, name=name + "_d", align_bytes=64)
-            nc.vector.tensor_copy(d[:], g[:].rearrange("p (m t) -> p t m", t=PACK))
+        def deal_scales(d, g):
+            nc.vector.tensor_copy(d[:].rearrange("p (t m) -> p t m", t=PACK), g[:].rearrange("p (m t) -> p t m", t=PACK))
             return d
 
         def gather_words(name, win, tag):
@@ -78,10 +73,9 @@ def tile_picked_zdejag_silu_po_kernel(tc, x_words, x_scales, e_words, e_scales, 
         h_codes = []
         h_scales = []
 
-        def quantise_h(raw, u, tag):
+        def quantise_h(raw, u, codes):
             hb = keep.tile([P, HALF, PACK], BF16, name="hb%d" % u, tag="hb%d" % u, align_bytes=64)
             interleave(nc.scalar.copy, hb[:], raw)
-            codes = keep.tile([P, HALF], U32, name="h_codes%d" % u, tag=tag, align_bytes=64)
             scales = keep.tile([P, HALF], U8, name="h_scales%d" % u, align_bytes=64)
             nc.vector.quantize_mx(out=codes[:].bitcast(FP8X4), scales=scales[:], in_=hb[:].rearrange("p j t -> p (j t)"))
             h_codes.append(codes)
@@ -91,27 +85,26 @@ def tile_picked_zdejag_silu_po_kernel(tc, x_words, x_scales, e_words, e_scales, 
             bank = psum.tile([P, 2, HALF], F32, name="%s%d%d" % (name, u, v), tag="%s%d%d" % (name, u, v))
             for i in range(2):
                 t = 2 * v + i
-                nc.tensor.matmul_mx(out=bank[:, i, :], lhsT=words[:, t, :].bitcast(FP8X4), lhsT_scale=scales[k:P, t, :],
+                nc.tensor.matmul_mx(out=bank[:, i, :], lhsT=words[:, t, :].bitcast(FP8X4), lhsT_scale=scales[k:P, t * P : (t + 1) * P],
                                     rhs=h_codes[u][:].bitcast(FP8X4), rhs_scale=h_scales[u][:], start=True, stop=True)
             return bank
 
-        def gate(y, u):
-            g = keep.tile([P, PACK, HALF], F32, name="gate%d" % u, tag="gate%d" % u)
-            for v in range(2):
-                nc.scalar.activation(g[:, 2 * v : 2 * v + 2, :], y[v][:], SILU)
-            return g
-
         xs_g = gather_scales("xs", xs_win)
-        quantise_h(h_a[:], 0, "xs_win")
-        xs = deal_scales("xs", xs_g)
-        xw = gather_words("xw", xw_win, "xw_g")
-        ys = [[product("y", xw, xs, 0, 0, v) for v in range(2)]]
         es_g = gather_scales("es", es_win)
-        es = deal_scales("es", es_g)
-        quantise_h(h_b[:], 1, "h_codes1")
-        ys.append([product("y", xw, xs, 0, 1, v) for v in range(2)])
-        gates = [gate(ys[u], u) for u in range(2)]
-        ew = gather_words("ew", ew_win, "hb1")
+        xs = deal_scales(laid.tile([P, S], U8, name="xs", align_bytes=64, offset=T), xs_g)
+        es = deal_scales(keep.tile([P, S], U8, name="es", align_bytes=64), es_g)
+        for r in range(1, 4):
+            nc.sync.dma_start(es[4 + r : P : 32, :].bitcast(I32), es[4 + 8 * r : P : 32, :].bitcast(I32))
+        quantise_h(h_raw[:, :, 0:HALF], 0, laid.tile([P, HALF], U32, name="h_codes0", align_bytes=64, offset=T + S))
+        xw = gather_words("xw", xw_win, "xw_g")
+        quantise_h(h_raw[:, :, HALF:J], 1, keep.tile([P, HALF], U32, name="h_codes1", tag="xw_win", align_bytes=64))
+        both = keep.tile([P, 2, PACK, HALF], F32, name="gates", tag="gates")
+        gates = [both[:, u] for u in range(2)]
+        for u in range(2):
+            for v in range(2):
+                y = product("y", xw, xs, 0, u, v)
+                nc.scalar.activation(gates[u][:, 2 * v : 2 * v + 2, :], y[:], SILU)
+        ew = gather_words("ew", ew_win, "ew_g")
 
         o_codes = keep.tile([P, J], U32, name="o_codes", align_bytes=64)
         o_scales = keep.tile([P, J], U8, name="o_scales", align_bytes=64)
@@ -132,7 +125,7 @@ def tile_picked_zdejag_silu_po_kernel(tc, x_words, x_scales, e_words, e_scales, 
 
         def one_plane(name, u, t):
             bank = psum.tile([P, HALF], F32, name=name, tag=name)
-            nc.tensor.matmul_mx(out=bank[:], lhsT=ew[:, t, :].bitcast(FP8X4), lhsT_scale=es[4:P, t, :],
+            nc.tensor.matmul_mx(out=bank[:], lhsT=ew[:, t, :].bitcast(FP8X4), lhsT_scale=es[4:P, t * P : (t + 1) * P],
                                 rhs=h_codes[u][:].bitcast(FP8X4), rhs_scale=h_scales[u][:], start=True, stop=True)
             return bank
 

@@ -40,13 +40,13 @@ def tile_picked_zdejag_silu_po_kernel(tc, x_words, x_scales, e_words, e_scales, 
         h_rows = hT.rearrange("(p t) j -> p t j", t=PACK)
         h_raw = keep.tile([P, PACK, J], F32, name="h_raw", tag="gates")
         nc.sync.dma_start(h_raw[:, 0:2, :], h_rows[:, 0:2, :])
+        es_win = keep.tile([P, T], U8, name="es_win", align_bytes=64)
+        nc.vector.memset(es_win[:].bitcast(I32), 0)
+        nc.sync.dma_start(es_win[4:P:8, :].bitcast(I32), e_scales[0].bitcast(I32))
         xs_win = laid.tile([P, T], U8, name="xs_win", align_bytes=64, offset=0)
-        nc.vector.memset(xs_win[:].bitcast(I32), 0)
+        nc.gpsimd.memset(xs_win[:].bitcast(I32), 0)
         for r in range(4):
             nc.sync.dma_start(xs_win[r:P:32, :].bitcast(I32), x_scales[0, r:16:4, :].bitcast(I32))
-        es_win = laid.tile([P, T], U8, name="es_win", align_bytes=64, offset=T)
-        nc.gpsimd.memset(es_win[:].bitcast(I32), 0)
-        nc.sync.dma_start(es_win[4:P:8, :].bitcast(I32), e_scales[0].bitcast(I32))
         nc.sync.dma_start(h_raw[:, 2:4, :], h_rows[:, 2:4, :])
         xw_win = load_words("xw_win", x_words)
         ew_win = load_words("ew_win", e_words)
@@ -89,13 +89,13 @@ def tile_picked_zdejag_silu_po_kernel(tc, x_words, x_scales, e_words, e_scales, 
                                     rhs=h_codes[u][:].bitcast(FP8X4), rhs_scale=h_scales[u][:], start=True, stop=True)
             return bank
 
-        xs_g = gather_scales("xs", xs_win)
         es_g = gather_scales("es", es_win)
-        xs = deal_scales(laid.tile([P, S], U8, name="xs", align_bytes=64, offset=T), xs_g)
-        es = deal_scales(keep.tile([P, S], U8, name="es", align_bytes=64), es_g)
+        xs_g = gather_scales("xs", xs_win)
+        es = deal_scales(laid.tile([P, S], U8, name="es", align_bytes=64, offset=0), es_g)
         for r in range(1, 4):
             nc.sync.dma_start(es[4 + r : P : 32, :].bitcast(I32), es[4 + 8 * r : P : 32, :].bitcast(I32))
-        quantise_h(h_raw[:, :, 0:HALF], 0, laid.tile([P, HALF], U32, name="h_codes0", align_bytes=64, offset=T + S))
+        xs = deal_scales(keep.tile([P, S], U8, name="xs", align_bytes=64), xs_g)
+        quantise_h(h_raw[:, :, 0:HALF], 0, laid.tile([P, HALF], U32, name="h_codes0", align_bytes=64, offset=S))
         xw = gather_words("xw", xw_win, "xw_g")
         quantise_h(h_raw[:, :, HALF:J], 1, keep.tile([P, HALF], U32, name="h_codes1", tag="xw_win", align_bytes=64))
         both = keep.tile([P, 2, PACK, HALF], F32, name="gates", tag="gates")

@@ -44,7 +44,7 @@ def tile_picked_zdejag_silu_po_kernel(tc, x_words, x_scales, e_words, e_scales, 
         nc.vector.memset(es_win[:].bitcast(I32), 0)
         nc.sync.dma_start(es_win[4:P:8, :].bitcast(I32), e_scales[0].bitcast(I32))
         xs_win = laid.tile([P, T], U8, name="xs_win", align_bytes=64, offset=0)
-        nc.gpsimd.memset(xs_win[:].bitcast(I32), 0)
+        nc.vector.memset(xs_win[:].bitcast(I32), 0)
         for r in range(4):
             nc.sync.dma_start(xs_win[r:P:32, :].bitcast(I32), x_scales[0, r:16:4, :].bitcast(I32))
         nc.sync.dma_start(h_raw[:, 2:4, :], h_rows[:, 2:4, :])

@@ -11,11 +11,13 @@ U8 = mybir.dt.uint8
 FP8X4 = mybir.dt.float8_e4m3fn_x4
 SILU = mybir.ActivationFunctionType.Silu
 MULT = mybir.AluOpType.mult
+ADD = mybir.AluOpType.add
 
 P = 128
 PACK = 4
 K, T, S, J = 512, 2048, 512, 512
 HALF = 256
+QUART = 128
 FLOPS = 2 * 2 * K * S * J
 
 
@@ -26,9 +28,6 @@ def tile_picked_zdejag_silu_po_kernel(tc, x_words, x_scales, e_words, e_scales, 
         laid = ctx.enter_context(tc.tile_pool(name="laid", bufs=1))
         psum = ctx.enter_context(tc.psum_pool(name="psum", bufs=1))
 
-        offsets = keep.tile([P, S // 16], U16, name="offsets")
-        nc.sync.dma_start(offsets[:], offs)
-
         def load_words(name, src):
             win = keep.tile([P, T], U32, name=name, tag=name, align_bytes=64)
             nc.sync.dma_start(win[:].bitcast(I32), src[0].rearrange("p n t -> p (n t)").bitcast(I32))
@@ -37,27 +36,7 @@ def tile_picked_zdejag_silu_po_kernel(tc, x_words, x_scales, e_words, e_scales, 
         def interleave(copy, dst, src):
             copy(dst.rearrange("p (c i) t -> p c t i", i=4), src.rearrange("p t (c i) -> p c t i", i=4))
 
-        h_rows = hT.rearrange("(p t) j -> p t j", t=PACK)
-        h_raw = keep.tile([P, PACK, J], F32, name="h_raw", tag="gates")
-        nc.sync.dma_start(h_raw[:, 0:2, :], h_rows[:, 0:2, :])
-        es_win = keep.tile([P, T], U8, name="es_win", align_bytes=64)
-        nc.vector.memset(es_win[:].bitcast(I32), 0)
-        nc.sync.dma_start(es_win[4:P:8, :].bitcast(I32), e_scales[0].bitcast(I32))
-        xs_win = laid.tile([P, T], U8, name="xs_win", align_bytes=64, offset=0)
-        nc.vector.memset(xs_win[:].bitcast(I32), 0)
-        for r in range(4):
-            nc.sync.dma_start(xs_win[r:P:32, :].bitcast(I32), x_scales[0, r:16:4, :].bitcast(I32))
-        nc.sync.dma_start(h_raw[:, 2:4, :], h_rows[:, 2:4, :])
-        xw_win = load_words("xw_win", x_words)
-        ew_win = load_words("ew_win", e_words)
-
-        warm = keep.tile([P, 8], F32, name="warm")
-        warm2 = keep.tile([P, 8], F32, name="warm2")
-        nc.vector.memset(warm[:], 0.0)
-        nc.scalar.activation(warm2[:], warm[:], SILU)
-
-        def gather_scales(name, win):
-            g = keep.tile([P, S], U8, name=name + "_g", align_bytes=64)
+        def gather_scales(g, win):
             nc.vector.tensor_copy(g[:], win[:].indirect(offsets[:]))
             return g
 
@@ -65,92 +44,123 @@ def tile_picked_zdejag_silu_po_kernel(tc, x_words, x_scales, e_words, e_scales, 
             nc.vector.tensor_copy(d[:].rearrange("p (t m) -> p t m", t=PACK), g[:].rearrange("p (m t) -> p t m", t=PACK))
             return d
 
-        def gather_words(name, win, tag):
-            g = keep.tile([P, PACK, P], U32, name=name + "_g", tag=tag, align_bytes=64)
+        def gather_words(g, win):
             nc.vector.tensor_copy(g[:].rearrange("p t m -> p m t"), win[:].indirect(offsets[:]))
             return g
 
-        h_codes = []
-        h_scales = []
+        def quantise(codes, scales, rounded):
+            nc.vector.quantize_mx(out=codes.bitcast(FP8X4), scales=scales, in_=rounded.rearrange("p j t -> p (j t)"))
 
-        def quantise_h(raw, u, codes):
-            hb = keep.tile([P, HALF, PACK], BF16, name="hb%d" % u, tag="hb%d" % u, align_bytes=64)
-            interleave(nc.scalar.copy, hb[:], raw)
-            scales = keep.tile([P, HALF], U8, name="h_scales%d" % u, align_bytes=64)
-            nc.vector.quantize_mx(out=codes[:].bitcast(FP8X4), scales=scales[:], in_=hb[:].rearrange("p j t -> p (j t)"))
-            h_codes.append(codes)
-            h_scales.append(scales)
-
-        def product(name, words, scales, k, u, v):
-            bank = psum.tile([P, 2, HALF], F32, name="%s%d%d" % (name, u, v), tag="%s%d%d" % (name, u, v))
-            for i in range(2):
-                t = 2 * v + i
+        def passes(tag, words, scales, k, planes, codes, cscales, width):
+            bank = psum.tile([P, len(planes), width], F32, name=tag, tag=tag)
+            for i, t in enumerate(planes):
                 nc.tensor.matmul_mx(out=bank[:, i, :], lhsT=words[:, t, :].bitcast(FP8X4), lhsT_scale=scales[k:P, t * P : (t + 1) * P],
-                                    rhs=h_codes[u][:].bitcast(FP8X4), rhs_scale=h_scales[u][:], start=True, stop=True)
+                                    rhs=codes.bitcast(FP8X4), rhs_scale=cscales, start=True, stop=True)
             return bank
 
-        es_g = gather_scales("es", es_win)
-        xs_g = gather_scales("xs", xs_win)
-        es = deal_scales(laid.tile([P, S], U8, name="es", align_bytes=64, offset=0), es_g)
-        for r in range(1, 4):
-            nc.sync.dma_start(es[4 + r : P : 32, :].bitcast(I32), es[4 + 8 * r : P : 32, :].bitcast(I32))
+        h_rows = hT.rearrange("(p t) j -> p t j", t=PACK)
+        out_rows = out_0.rearrange("(p t) j -> p t j", t=PACK)
+        out_words = out_1[0].rearrange("p n t -> p (n t)").bitcast(I32)
+
+        offsets = keep.tile([P, S // 16], U16, name="offsets")
+        nc.sync.dma_start(offsets[:], offs)
+        xs_win = keep.tile([P, T], U8, name="xs_win", tag="xs_win", align_bytes=64)
+        es_win = keep.tile([P, T], U8, name="es_win", align_bytes=64)
+        nc.vector.memset(xs_win[:].bitcast(I32), 0)
+        nc.vector.memset(es_win[0:112, :].bitcast(I32), 0)
+        nc.sync.dma_start(es_win[112:P, :].bitcast(I32), e_scales[0].bitcast(I32))
+        h_a = keep.tile([P, PACK, HALF], F32, name="h_a")
+        nc.sync.dma_start(h_a[:], h_rows[:, :, 0:HALF])
+        for r in range(4):
+            nc.sync.dma_start(xs_win[r:P:32, :].bitcast(I32), x_scales[0, r:16:4, :].bitcast(I32))
+        xw_win = load_words("xw_win", x_words)
+        h_b = keep.tile([P, PACK, HALF], F32, name="h_b", tag="gates0")
+        nc.sync.dma_start(h_b[:], h_rows[:, :, HALF:J])
+        ew_win = load_words("ew_win", e_words)
+
+        warm = keep.tile([P, 8], F32, name="warm")
+        warm2 = keep.tile([P, 8], F32, name="warm2")
+        nc.vector.memset(warm[:], 0.0)
+        nc.scalar.activation(warm2[:], warm[:], SILU)
+
+        es_g = gather_scales(keep.tile([P, S], U8, name="es_g", align_bytes=64), es_win)
+        es = deal_scales(keep.tile([P, S], U8, name="es", align_bytes=64), es_g)
+        for r in range(4):
+            nc.sync.dma_start(es[4 + r : P : 32, :].bitcast(I32), es[112 + r : P : 4, :].bitcast(I32))
+        xs_g = gather_scales(keep.tile([P, S], U8, name="xs_g", align_bytes=64), xs_win)
         xs = deal_scales(keep.tile([P, S], U8, name="xs", align_bytes=64), xs_g)
-        quantise_h(h_raw[:, :, 0:HALF], 0, laid.tile([P, HALF], U32, name="h_codes0", align_bytes=64, offset=S))
-        xw = gather_words("xw", xw_win, "xw_g")
-        quantise_h(h_raw[:, :, HALF:J], 1, keep.tile([P, HALF], U32, name="h_codes1", tag="xw_win", align_bytes=64))
-        both = keep.tile([P, 2, PACK, HALF], F32, name="gates", tag="gates")
-        gates = [both[:, u] for u in range(2)]
+
+        h_codes = [keep.tile([P, HALF], U32, name="h_codes0", tag="xs_win", align_bytes=64), keep.tile([P, HALF], U32, name="h_codes1", align_bytes=64)]
+        h_scales = [keep.tile([P, HALF], U8, name="h_scales%d" % u, align_bytes=64) for u in range(2)]
+
+        def prepare(u, raw):
+            hb = keep.tile([P, HALF, PACK], BF16, name="hb%d" % u, align_bytes=64)
+            interleave(nc.scalar.copy, hb[:], raw[:])
+            quantise(h_codes[u][:], h_scales[u][:], hb[:])
+
+        prepare(0, h_a)
+        xw = gather_words(keep.tile([P, PACK, P], U32, name="xw", align_bytes=64), xw_win)
+        prepare(1, h_b)
+        gates = [keep.tile([P, PACK, HALF], F32, name="gates0", tag="gates0"), keep.tile([P, PACK, HALF], F32, name="gates1")]
         for u in range(2):
             for v in range(2):
-                y = product("y", xw, xs, 0, u, v)
+                y = passes("y%d%d" % (u, v), xw, xs, 0, (2 * v, 2 * v + 1), h_codes[u][:], h_scales[u][:], HALF)
                 nc.scalar.activation(gates[u][:, 2 * v : 2 * v + 2, :], y[:], SILU)
-        ew = gather_words("ew", ew_win, "ew_g")
+        ew = gather_words(keep.tile([P, PACK, P], U32, name="ew", align_bytes=64), ew_win)
 
         o_codes = keep.tile([P, J], U32, name="o_codes", align_bytes=64)
         o_scales = keep.tile([P, J], U8, name="o_scales", align_bytes=64)
-        out_rows = out_0.rearrange("(p t) j -> p t j", t=PACK)
-        out_words = out_1[0].rearrange("p n t -> p (n t)").bitcast(I32)
-        rounded = []
-
         o = [keep.tile([P, PACK, HALF], F32, name="o%d" % u) for u in range(2)]
+        ob = [keep.tile([P, HALF, PACK], BF16, name="ob%d" % u, align_bytes=64) for u in range(2)]
+        LO, HI, ALL = slice(0, 128), slice(128, 256), slice(0, 256)
 
-        def store(u, v):
-            nc.sync.dma_start(out_rows[:, 2 * v : 2 * v + 2, u * HALF : (u + 1) * HALF], o[u][:, 2 * v : 2 * v + 2, :])
-
-        def multiply(u, v):
-            e = product("e", ew, es, 4, u, v)
-            rows = slice(2 * v, 2 * v + 2)
-            nc.vector.tensor_tensor(o[u][:, rows, :], e[:], gates[u][:, rows, :], MULT)
-            store(u, v)
-
-        def one_plane(name, u, t):
-            bank = psum.tile([P, HALF], F32, name=name, tag=name)
-            nc.tensor.matmul_mx(out=bank[:], lhsT=ew[:, t, :].bitcast(FP8X4), lhsT_scale=es[4:P, t * P : (t + 1) * P],
-                                rhs=h_codes[u][:].bitcast(FP8X4), rhs_scale=h_scales[u][:], start=True, stop=True)
+        def values(tag, u, planes, cols):
+            bank = psum.tile([P, planes.stop - planes.start, cols.stop - cols.start], F32, name=tag, tag=tag)
+            for t in range(planes.start, planes.stop):
+                nc.tensor.matmul_mx(out=bank[:, t - planes.start, :], lhsT=ew[:, t, :].bitcast(FP8X4), lhsT_scale=es[4:P, t * P : (t + 1) * P],
+                                    rhs=h_codes[u][:, cols].bitcast(FP8X4), rhs_scale=h_scales[u][:, cols], start=True, stop=True)
             return bank
 
-        for t in range(2):
-            e_first = one_plane("e_first%d" % t, 0, t)
-            nc.vector.tensor_tensor(o[0][:, t, :], e_first[:], gates[0][:, t, :], MULT)
-            nc.sync.dma_start(out_rows[:, t, 0:HALF], o[0][:, t, :])
-        e_side = one_plane("y01", 1, 3)
-        e_sbuf = keep.tile([P, HALF], F32, name="e_sbuf")
+        def multiply(tag, u, planes, cols):
+            nc.vector.tensor_tensor(o[u][:, planes, cols], values(tag, u, planes, cols)[:], gates[u][:, planes, cols], MULT)
+
+        def store(u, planes, cols):
+            nc.sync.dma_start(out_rows[:, planes, u * HALF + cols.start : u * HALF + cols.stop], o[u][:, planes, cols])
+
+        def round_out(copy, u, cols):
+            interleave(copy, ob[u][:, cols, :], o[u][:, :, cols])
+
+        def quantise_out(u, cols):
+            at = slice(u * HALF + cols.start, u * HALF + cols.stop)
+            nc.vector.quantize_mx(out=o_codes[:, at].bitcast(FP8X4), scales=o_scales[:, at], in_=ob[u][:, cols, :].rearrange("p j t -> p (j t)"))
+
+        def store_words(u):
+            at = slice(u * HALF, (u + 1) * HALF)
+            nc.sync.dma_start(out_words[:, at], o_codes[:, at].bitcast(I32))
+
+        T01, T23, T03 = slice(0, 2), slice(2, 4), slice(0, 4)
+        multiply("ea", 0, T01, LO)
+        multiply("eb", 0, T23, LO)
+        store(0, T03, LO)
+        e_side = values("y01", 1, T23, LO)
+        e_sbuf = keep.tile([P, 2, 128], F32, name="e_sbuf")
         nc.scalar.copy(e_sbuf[:], e_side[:])
-        nc.gpsimd.tensor_tensor(o[1][:, 3, :], e_sbuf[:], gates[1][:, 3, :], MULT)
-        multiply(0, 1)
-        multiply(1, 0)
-        e_last = one_plane("y00", 1, 2)
-        nc.vector.tensor_tensor(o[1][:, 2, :], e_last[:], gates[1][:, 2, :], MULT)
-        store(1, 1)
-        for u, split in enumerate((192, 80)):
-            b = keep.tile([P, HALF, PACK], BF16, name="ob%d" % u, align_bytes=64)
-            interleave(nc.scalar.copy, b[:, 0:split, :], o[u][:, :, 0:split])
-            interleave(nc.vector.tensor_copy, b[:, split:HALF, :], o[u][:, :, split:HALF])
-            rounded.append(b)
-        for u in range(2):
-            cols = slice(u * HALF, (u + 1) * HALF)
-            nc.vector.quantize_mx(out=o_codes[:, cols].bitcast(FP8X4), scales=o_scales[:, cols], in_=rounded[u][:].rearrange("p j t -> p (j t)"))
-            nc.sync.dma_start(out_words[:, cols], o_codes[:, cols].bitcast(I32))
+        nc.gpsimd.tensor_tensor(o[1][:, T23, LO], e_sbuf[:], gates[1][:, T23, LO], MULT)
+        round_out(nc.scalar.copy, 0, LO)
+        multiply("ec", 0, T03, HI)
+        store(0, T03, HI)
+        round_out(nc.scalar.copy, 0, HI)
+        multiply("ed", 1, T01, ALL)
+        store(1, T01, ALL)
+        round_out(nc.scalar.copy, 1, LO)
+        multiply("y00", 1, T23, HI)
+        store(1, T23, ALL)
+        quantise_out(0, ALL)
+        store_words(0)
+        round_out(nc.vector.tensor_copy, 1, HI)
+        quantise_out(1, LO)
+        quantise_out(1, HI)
+        store_words(1)
         for r in range(4):
             eng = nc.scalar if r % 2 == 0 else nc.sync
             eng.dma_start(out_2[0, r:16:4, :].bitcast(I32), o_scales[r:P:32, :].bitcast(I32))

@@ -64,33 +64,34 @@ def tile_picked_zdejag_silu_po_kernel(tc, x_words, x_scales, e_words, e_scales, 
 
         offsets = keep.tile([P, S // 16], U16, name="offsets")
         nc.sync.dma_start(offsets[:], offs)
-        xs_win = keep.tile([P, T], U8, name="xs_win", tag="xs_win", align_bytes=64)
-        es_win = keep.tile([P, T], U8, name="es_win", align_bytes=64)
-        nc.vector.memset(xs_win[:].bitcast(I32), 0)
-        nc.vector.memset(es_win[0:112, :].bitcast(I32), 0)
-        nc.sync.dma_start(es_win[112:P, :].bitcast(I32), e_scales[0].bitcast(I32))
+        xs_win = keep.tile([P, T], U8, name="xs_win", align_bytes=64)
+        es_win = keep.tile([P, T], U8, name="es_win", tag="es_win", align_bytes=64)
+        nc.vector.memset(es_win[:].bitcast(I32), 0)
+        nc.vector.memset(xs_win[0:112, :].bitcast(I32), 0)
+        nc.sync.dma_start(xs_win[112:P, :].bitcast(I32), x_scales[0].bitcast(I32))
         h_a = keep.tile([P, PACK, HALF], F32, name="h_a")
         nc.sync.dma_start(h_a[:], h_rows[:, :, 0:HALF])
-        for r in range(4):
-            nc.sync.dma_start(xs_win[r:P:32, :].bitcast(I32), x_scales[0, r:16:4, :].bitcast(I32))
+        nc.sync.dma_start(es_win[4:P:8, :].bitcast(I32), e_scales[0].bitcast(I32))
         xw_win = load_words("xw_win", x_words)
         h_b = keep.tile([P, PACK, HALF], F32, name="h_b", tag="gates0")
         nc.sync.dma_start(h_b[:], h_rows[:, :, HALF:J])
-        ew_win = load_words("ew_win", e_words)
 
         warm = keep.tile([P, 8], F32, name="warm")
         warm2 = keep.tile([P, 8], F32, name="warm2")
         nc.vector.memset(warm[:], 0.0)
         nc.scalar.activation(warm2[:], warm[:], SILU)
 
+        xs_g = gather_scales(keep.tile([P, S], U8, name="xs_g", tag="ew_win", align_bytes=64), xs_win)
+        xs = deal_scales(keep.tile([P, S], U8, name="xs", align_bytes=64), xs_g)
+        for r in range(4):
+            nc.sync.dma_start(xs[r:P:32, :].bitcast(I32), xs[112 + r : P : 4, :].bitcast(I32))
+        ew_win = load_words("ew_win", e_words)
         es_g = gather_scales(keep.tile([P, S], U8, name="es_g", align_bytes=64), es_win)
         es = deal_scales(keep.tile([P, S], U8, name="es", align_bytes=64), es_g)
-        for r in range(4):
-            nc.sync.dma_start(es[4 + r : P : 32, :].bitcast(I32), es[112 + r : P : 4, :].bitcast(I32))
-        xs_g = gather_scales(keep.tile([P, S], U8, name="xs_g", align_bytes=64), xs_win)
-        xs = deal_scales(keep.tile([P, S], U8, name="xs", align_bytes=64), xs_g)
+        for r in range(1, 4):
+            nc.sync.dma_start(es[4 + r : P : 32, :].bitcast(I32), es[4 + 8 * r : P : 32, :].bitcast(I32))
 
-        h_codes = [keep.tile([P, HALF], U32, name="h_codes0", tag="xs_win", align_bytes=64), keep.tile([P, HALF], U32, name="h_codes1", align_bytes=64)]
+        h_codes = [keep.tile([P, HALF], U32, name="h_codes0", tag="es_win", align_bytes=64), keep.tile([P, HALF], U32, name="h_codes1", align_bytes=64)]
         h_scales = [keep.tile([P, HALF], U8, name="h_scales%d" % u, align_bytes=64) for u in range(2)]
 
         def prepare(u, raw):
@@ -139,27 +140,27 @@ def tile_picked_zdejag_silu_po_kernel(tc, x_words, x_scales, e_words, e_scales, 
             nc.sync.dma_start(out_words[:, at], o_codes[:, at].bitcast(I32))
 
         T01, T23, T03 = slice(0, 2), slice(2, 4), slice(0, 4)
-        multiply("ea", 0, T01, LO)
-        multiply("eb", 0, T23, LO)
-        store(0, T03, LO)
-        e_side = values("y01", 1, T23, LO)
-        e_sbuf = keep.tile([P, 2, 128], F32, name="e_sbuf")
+        multiply("ea", 0, slice(0, 1), ALL)
+        store(0, slice(0, 1), ALL)
+        multiply("eb", 0, slice(1, 2), ALL)
+        store(0, slice(1, 2), ALL)
+        e_side = values("y01", 1, slice(3, 4), ALL)
+        e_sbuf = keep.tile([P, 1, 256], F32, name="e_sbuf")
         nc.scalar.copy(e_sbuf[:], e_side[:])
-        nc.gpsimd.tensor_tensor(o[1][:, T23, LO], e_sbuf[:], gates[1][:, T23, LO], MULT)
-        round_out(nc.scalar.copy, 0, LO)
-        multiply("ec", 0, T03, HI)
-        store(0, T03, HI)
-        round_out(nc.scalar.copy, 0, HI)
+        nc.gpsimd.tensor_tensor(o[1][:, 3:4, :], e_sbuf[:], gates[1][:, 3:4, :], MULT)
+        multiply("ec", 0, T23, ALL)
+        store(0, T23, ALL)
         multiply("ed", 1, T01, ALL)
         store(1, T01, ALL)
-        round_out(nc.scalar.copy, 1, LO)
-        multiply("y00", 1, T23, HI)
+        multiply("y00", 1, slice(2, 3), ALL)
         store(1, T23, ALL)
+        round_out(nc.scalar.copy, 0, slice(0, 192))
+        round_out(nc.vector.tensor_copy, 0, slice(192, 256))
+        round_out(nc.scalar.copy, 1, slice(0, 80))
+        round_out(nc.vector.tensor_copy, 1, slice(80, 256))
         quantise_out(0, ALL)
         store_words(0)
-        round_out(nc.vector.tensor_copy, 1, HI)
-        quantise_out(1, LO)
-        quantise_out(1, HI)
+        quantise_out(1, ALL)
         store_words(1)
         for r in range(4):
             eng = nc.scalar if r % 2 == 0 else nc.sync

@@ -123,7 +123,7 @@ def tile_picked_zdejag_silu_po_kernel(tc, x_words, x_scales, e_words, e_scales, 
             return bank
 
         def multiply(tag, u, planes, cols):
-            nc.vector.tensor_tensor(o[u][:, planes, cols], values(tag, u, planes, cols)[:], gates[u][:, planes, cols], MULT)
+            nc.vector.tensor_tensor(o[u][:, planes, cols], gates[u][:, planes, cols], values(tag, u, planes, cols)[:], MULT)
 
         def store(u, planes, cols):
             nc.sync.dma_start(out_rows[:, planes, u * HALF + cols.start : u * HALF + cols.stop], o[u][:, planes, cols])

@@ -64,11 +64,11 @@ def tile_picked_zdejag_silu_po_kernel(tc, x_words, x_scales, e_words, e_scales, 
 
         offsets = keep.tile([P, S // 16], U16, name="offsets")
         nc.sync.dma_start(offsets[:], offs)
-        xs_win = keep.tile([P, T], U8, name="xs_win", align_bytes=64)
+        xs_win = keep.tile([P, T], U8, name="xs_win", tag="ew_win", align_bytes=64)
         es_win = keep.tile([P, T], U8, name="es_win", tag="es_win", align_bytes=64)
         nc.vector.memset(es_win[:].bitcast(I32), 0)
         nc.vector.memset(xs_win[0:112, :].bitcast(I32), 0)
-        nc.sync.dma_start(xs_win[112:P, :].bitcast(I32), x_scales[0].bitcast(I32))
+        nc.scalar.dma_start(xs_win[112:P, :].bitcast(I32), x_scales[0].bitcast(I32))
         h_a = keep.tile([P, PACK, HALF], F32, name="h_a")
         nc.sync.dma_start(h_a[:], h_rows[:, :, 0:HALF])
         nc.sync.dma_start(es_win[4:P:8, :].bitcast(I32), e_scales[0].bitcast(I32))
@@ -81,17 +81,18 @@ def tile_picked_zdejag_silu_po_kernel(tc, x_words, x_scales, e_words, e_scales, 
         nc.vector.memset(warm[:], 0.0)
         nc.scalar.activation(warm2[:], warm[:], SILU)
 
-        xs_g = gather_scales(keep.tile([P, S], U8, name="xs_g", tag="ew_win", align_bytes=64), xs_win)
-        xs = deal_scales(keep.tile([P, S], U8, name="xs", align_bytes=64), xs_g)
+        xs_m = keep.tile([P, S], U8, name="xs_m", tag="xs_m", align_bytes=64)
+        nc.vector.memset(xs_m[:].bitcast(I32), 0)
+        xs_g = gather_scales(keep.tile([P, S], U8, name="xs_g", align_bytes=64), xs_win)
         for r in range(4):
-            nc.sync.dma_start(xs[r:P:32, :].bitcast(I32), xs[112 + r : P : 4, :].bitcast(I32))
+            nc.sync.dma_start(xs_m[r:P:32, :].bitcast(I32), xs_g[112 + r : P : 4, :].bitcast(I32))
         ew_win = load_words("ew_win", e_words)
         es_g = gather_scales(keep.tile([P, S], U8, name="es_g", align_bytes=64), es_win)
         es = deal_scales(keep.tile([P, S], U8, name="es", align_bytes=64), es_g)
         for r in range(1, 4):
             nc.sync.dma_start(es[4 + r : P : 32, :].bitcast(I32), es[4 + 8 * r : P : 32, :].bitcast(I32))
 
-        h_codes = [keep.tile([P, HALF], U32, name="h_codes0", tag="es_win", align_bytes=64), keep.tile([P, HALF], U32, name="h_codes1", align_bytes=64)]
+        h_codes = [keep.tile([P, HALF], U32, name="h_codes0", tag="es_win", align_bytes=64), keep.tile([P, HALF], U32, name="h_codes1", tag="xs_m", align_bytes=64)]
         h_scales = [keep.tile([P, HALF], U8, name="h_scales%d" % u, align_bytes=64) for u in range(2)]
 
         def prepare(u, raw):
@@ -101,6 +102,7 @@ def tile_picked_zdejag_silu_po_kernel(tc, x_words, x_scales, e_words, e_scales, 
 
         prepare(0, h_a)
         xw = gather_words(keep.tile([P, PACK, P], U32, name="xw", align_bytes=64), xw_win)
+        xs = deal_scales(keep.tile([P, S], U8, name="xs", align_bytes=64), xs_m)
         prepare(1, h_b)
         gates = [keep.tile([P, PACK, HALF], F32, name="gates0", tag="gates0"), keep.tile([P, PACK, HALF], F32, name="gates1")]
         for u in range(2):
@@ -139,25 +141,28 @@ def tile_picked_zdejag_silu_po_kernel(tc, x_words, x_scales, e_words, e_scales, 
             at = slice(u * HALF, (u + 1) * HALF)
             nc.sync.dma_start(out_words[:, at], o_codes[:, at].bitcast(I32))
 
-        T01, T23, T03 = slice(0, 2), slice(2, 4), slice(0, 4)
-        multiply("ea", 0, slice(0, 1), ALL)
-        store(0, slice(0, 1), ALL)
-        multiply("eb", 0, slice(1, 2), ALL)
-        store(0, slice(1, 2), ALL)
-        e_side = values("y01", 1, slice(3, 4), ALL)
-        e_sbuf = keep.tile([P, 1, 256], F32, name="e_sbuf")
+        T0, T1, T01, T23 = slice(0, 1), slice(1, 2), slice(0, 2), slice(2, 4)
+        multiply("ea", 0, T0, ALL)
+        store(0, T0, ALL)
+        multiply("eb", 0, T1, ALL)
+        store(0, T1, ALL)
+        e_side = values("ec", 1, T23, LO)
+        e_sbuf = keep.tile([P, 2, 128], F32, name="e_sbuf")
         nc.scalar.copy(e_sbuf[:], e_side[:])
-        nc.gpsimd.tensor_tensor(o[1][:, 3:4, :], e_sbuf[:], gates[1][:, 3:4, :], MULT)
-        multiply("ec", 0, T23, ALL)
+        nc.gpsimd.tensor_tensor(o[1][:, T23, LO], e_sbuf[:], gates[1][:, T23, LO], MULT)
+        multiply("ed", 0, T23, LO)
+        round_out(nc.scalar.copy, 0, LO)
+        multiply("y00", 0, T23, HI)
         store(0, T23, ALL)
-        multiply("ed", 1, T01, ALL)
+        round_out(nc.scalar.copy, 0, HI)
+        multiply("y01", 1, T0, ALL)
+        multiply("y10", 1, T1, ALL)
         store(1, T01, ALL)
-        multiply("y00", 1, slice(2, 3), ALL)
+        multiply("y11", 1, T23, HI)
         store(1, T23, ALL)
-        round_out(nc.scalar.copy, 0, slice(0, 192))
-        round_out(nc.vector.tensor_copy, 0, slice(192, 256))
-        round_out(nc.scalar.copy, 1, slice(0, 80))
-        round_out(nc.vector.tensor_copy, 1, slice(80, 256))
+        round_out(nc.vector.tensor_copy, 1, LO)
+        round_out(nc.scalar.copy, 1, slice(128, 192))
+        round_out(nc.vector.tensor_copy, 1, slice(192, 256))
         quantise_out(0, ALL)
         store_words(0)
         quantise_out(1, ALL)

@@ -81,18 +81,20 @@ def tile_picked_zdejag_silu_po_kernel(tc, x_words, x_scales, e_words, e_scales, 
         nc.vector.memset(warm[:], 0.0)
         nc.scalar.activation(warm2[:], warm[:], SILU)
 
-        xs_m = keep.tile([P, S], U8, name="xs_m", tag="xs_m", align_bytes=64)
-        nc.vector.memset(xs_m[:].bitcast(I32), 0)
-        xs_g = gather_scales(keep.tile([P, S], U8, name="xs_g", align_bytes=64), xs_win)
+        xs = keep.tile([P, S], U8, name="xs", align_bytes=64)
+        nc.vector.memset(xs[:].bitcast(I32), 0)
+        xs_g = keep.tile([P, S], U8, name="xs_g", align_bytes=64)
+        nc.vector.tensor_copy(xs_g[:].rearrange("p (t m) -> p m t", t=PACK), xs_win[:].indirect(offsets[:]))
         for r in range(4):
-            nc.sync.dma_start(xs_m[r:P:32, :].bitcast(I32), xs_g[112 + r : P : 4, :].bitcast(I32))
+            eng = nc.scalar if r == 0 else nc.sync
+            eng.dma_start(xs[r:P:32, :].bitcast(I32), xs_g[112 + r : P : 4, :].bitcast(I32))
         ew_win = load_words("ew_win", e_words)
         es_g = gather_scales(keep.tile([P, S], U8, name="es_g", align_bytes=64), es_win)
         es = deal_scales(keep.tile([P, S], U8, name="es", align_bytes=64), es_g)
         for r in range(1, 4):
             nc.sync.dma_start(es[4 + r : P : 32, :].bitcast(I32), es[4 + 8 * r : P : 32, :].bitcast(I32))
 
-        h_codes = [keep.tile([P, HALF], U32, name="h_codes0", tag="es_win", align_bytes=64), keep.tile([P, HALF], U32, name="h_codes1", tag="xs_m", align_bytes=64)]
+        h_codes = [keep.tile([P, HALF], U32, name="h_codes0", tag="es_win", align_bytes=64), keep.tile([P, HALF], U32, name="h_codes1", align_bytes=64)]
         h_scales = [keep.tile([P, HALF], U8, name="h_scales%d" % u, align_bytes=64) for u in range(2)]
 
         def prepare(u, raw):
@@ -102,8 +104,10 @@ def tile_picked_zdejag_silu_po_kernel(tc, x_words, x_scales, e_words, e_scales, 
 
         prepare(0, h_a)
         xw = gather_words(keep.tile([P, PACK, P], U32, name="xw", align_bytes=64), xw_win)
-        xs = deal_scales(keep.tile([P, S], U8, name="xs", align_bytes=64), xs_m)
-        prepare(1, h_b)
+        hb1 = keep.tile([P, HALF, PACK], BF16, name="hb1", align_bytes=64)
+        interleave(nc.scalar.copy, hb1[:, 0:144, :], h_b[:, :, 0:144])
+        interleave(nc.vector.tensor_copy, hb1[:, 144:HALF, :], h_b[:, :, 144:HALF])
+        quantise(h_codes[1][:], h_scales[1][:], hb1[:])
         gates = [keep.tile([P, PACK, HALF], F32, name="gates0", tag="gates0"), keep.tile([P, PACK, HALF], F32, name="gates1")]
         for u in range(2):
             for v in range(2):
@@ -113,7 +117,8 @@ def tile_picked_zdejag_silu_po_kernel(tc, x_words, x_scales, e_words, e_scales, 
 
         o_codes = keep.tile([P, J], U32, name="o_codes", align_bytes=64)
         o_scales = keep.tile([P, J], U8, name="o_scales", align_bytes=64)
-        o = [keep.tile([P, PACK, HALF], F32, name="o%d" % u) for u in range(2)]
+        o_all = keep.tile([P, PACK, J], F32, name="o_all")
+        o = [o_all[:, :, u * HALF : (u + 1) * HALF] for u in range(2)]
         ob = [keep.tile([P, HALF, PACK], BF16, name="ob%d" % u, align_bytes=64) for u in range(2)]
         LO, HI, ALL = slice(0, 128), slice(128, 256), slice(0, 256)
 
@@ -141,7 +146,7 @@ def tile_picked_zdejag_silu_po_kernel(tc, x_words, x_scales, e_words, e_scales, 
             at = slice(u * HALF, (u + 1) * HALF)
             nc.sync.dma_start(out_words[:, at], o_codes[:, at].bitcast(I32))
 
-        T0, T1, T01, T23 = slice(0, 1), slice(1, 2), slice(0, 2), slice(2, 4)
+        T0, T1, T2, T01, T23 = slice(0, 1), slice(1, 2), slice(2, 3), slice(0, 2), slice(2, 4)
         multiply("ea", 0, T0, ALL)
         store(0, T0, ALL)
         multiply("eb", 0, T1, ALL)
@@ -153,13 +158,14 @@ def tile_picked_zdejag_silu_po_kernel(tc, x_words, x_scales, e_words, e_scales, 
         multiply("ed", 0, T23, LO)
         round_out(nc.scalar.copy, 0, LO)
         multiply("y00", 0, T23, HI)
-        store(0, T23, ALL)
+        store(0, T2, ALL)
         round_out(nc.scalar.copy, 0, HI)
-        multiply("y01", 1, T0, ALL)
-        multiply("y10", 1, T1, ALL)
+        multiply("y01", 1, T23, HI)
+        run = slice(2 * J + HALF, PACK * J)
+        nc.sync.dma_start(out_0.rearrange("(p t) j -> p (t j)", t=PACK)[:, run], o_all[:].rearrange("p t j -> p (t j)")[:, run])
+        multiply("y10", 1, T01, LO)
+        multiply("y11", 1, T01, HI)
         store(1, T01, ALL)
-        multiply("y11", 1, T23, HI)
-        store(1, T23, ALL)
         round_out(nc.vector.tensor_copy, 1, LO)
         round_out(nc.scalar.copy, 1, slice(128, 192))
         round_out(nc.vector.tensor_copy, 1, slice(192, 256))

@@ -147,24 +147,25 @@ def tile_picked_zdejag_silu_po_kernel(tc, x_words, x_scales, e_words, e_scales, 
             nc.sync.dma_start(out_words[:, at], o_codes[:, at].bitcast(I32))
 
         T0, T1, T2, T01, T23 = slice(0, 1), slice(1, 2), slice(2, 3), slice(0, 2), slice(2, 4)
-        multiply("ea", 0, T0, ALL)
+        multiply("ea", 0, T0, LO)
+        multiply("eb", 0, T0, HI)
         store(0, T0, ALL)
-        multiply("eb", 0, T1, ALL)
+        multiply("ec", 0, T1, ALL)
         store(0, T1, ALL)
-        e_side = values("ec", 1, T23, LO)
+        e_side = values("ed", 1, T23, LO)
         e_sbuf = keep.tile([P, 2, 128], F32, name="e_sbuf")
         nc.scalar.copy(e_sbuf[:], e_side[:])
         nc.gpsimd.tensor_tensor(o[1][:, T23, LO], e_sbuf[:], gates[1][:, T23, LO], MULT)
-        multiply("ed", 0, T23, LO)
+        multiply("y00", 0, T23, LO)
         round_out(nc.scalar.copy, 0, LO)
-        multiply("y00", 0, T23, HI)
+        multiply("y01", 0, T23, HI)
         store(0, T2, ALL)
         round_out(nc.scalar.copy, 0, HI)
-        multiply("y01", 1, T23, HI)
+        multiply("y10", 1, T23, HI)
         run = slice(2 * J + HALF, PACK * J)
         nc.sync.dma_start(out_0.rearrange("(p t) j -> p (t j)", t=PACK)[:, run], o_all[:].rearrange("p t j -> p (t j)")[:, run])
-        multiply("y10", 1, T01, LO)
-        multiply("y11", 1, T01, HI)
+        multiply("y11", 1, T01, LO)
+        multiply("ea", 1, T01, HI)
         store(1, T01, ALL)
         round_out(nc.vector.tensor_copy, 1, LO)
         round_out(nc.scalar.copy, 1, slice(128, 192))

from contextlib import ExitStack

import concourse.mybir as mybir

F32 = mybir.dt.float32
BF16 = mybir.dt.bfloat16
I32 = mybir.dt.int32
U32 = mybir.dt.uint32
U16 = mybir.dt.uint16
U8 = mybir.dt.uint8
FP8X4 = mybir.dt.float8_e4m3fn_x4
SILU = mybir.ActivationFunctionType.Silu
MULT = mybir.AluOpType.mult
ADD = mybir.AluOpType.add

P = 128
PACK = 4
K, T, S, J = 512, 2048, 512, 512
HALF = 256
QUART = 128
FLOPS = 2 * 2 * K * S * J


def tile_picked_zdejag_silu_po_kernel(tc, x_words, x_scales, e_words, e_scales, hT, offs, out_0, out_1, out_2):
    nc = tc.nc
    with ExitStack() as ctx:
        keep = ctx.enter_context(tc.tile_pool(name="keep", bufs=1))
        laid = ctx.enter_context(tc.tile_pool(name="laid", bufs=1))
        psum = ctx.enter_context(tc.psum_pool(name="psum", bufs=1))

        def load_words(name, src):
            win = keep.tile([P, T], U32, name=name, tag=name, align_bytes=64)
            nc.sync.dma_start(win[:].bitcast(I32), src[0].rearrange("p n t -> p (n t)").bitcast(I32))
            return win

        def interleave(copy, dst, src):
            copy(dst.rearrange("p (c i) t -> p c t i", i=4), src.rearrange("p t (c i) -> p c t i", i=4))

        def gather_scales(g, win):
            nc.vector.tensor_copy(g[:], win[:].indirect(offsets[:]))
            return g

        def deal_scales(d, g):
            nc.vector.tensor_copy(d[:].rearrange("p (t m) -> p t m", t=PACK), g[:].rearrange("p (m t) -> p t m", t=PACK))
            return d

        def gather_words(g, win):
            nc.vector.tensor_copy(g[:].rearrange("p t m -> p m t"), win[:].indirect(offsets[:]))
            return g

        def quantise(codes, scales, rounded):
            nc.vector.quantize_mx(out=codes.bitcast(FP8X4), scales=scales, in_=rounded.rearrange("p j t -> p (j t)"))

        def passes(tag, words, scales, k, planes, codes, cscales, width):
            bank = psum.tile([P, len(planes), width], F32, name=tag, tag=tag)
            for i, t in enumerate(planes):
                nc.tensor.matmul_mx(out=bank[:, i, :], lhsT=words[:, t, :].bitcast(FP8X4), lhsT_scale=scales[k:P, t * P : (t + 1) * P],
                                    rhs=codes.bitcast(FP8X4), rhs_scale=cscales, start=True, stop=True)
            return bank

        h_rows = hT.rearrange("(p t) j -> p t j", t=PACK)
        out_rows = out_0.rearrange("(p t) j -> p t j", t=PACK)
        out_words = out_1[0].rearrange("p n t -> p (n t)").bitcast(I32)

        offsets = keep.tile([P, S // 16], U16, name="offsets")
        nc.sync.dma_start(offsets[:], offs)
        xs_win = keep.tile([P, T], U8, name="xs_win", tag="ew_win", align_bytes=64)
        es_win = keep.tile([P, T], U8, name="es_win", tag="es_win", align_bytes=64)
        nc.vector.memset(es_win[:].bitcast(I32), 0)
        nc.vector.memset(xs_win[0:112, :].bitcast(I32), 0)
        nc.scalar.dma_start(xs_win[112:P, :].bitcast(I32), x_scales[0].bitcast(I32))
        h_a = keep.tile([P, PACK, HALF], F32, name="h_a")
        nc.sync.dma_start(h_a[:], h_rows[:, :, 0:HALF])
        nc.sync.dma_start(es_win[4:P:8, :].bitcast(I32), e_scales[0].bitcast(I32))
        xw_win = load_words("xw_win", x_words)
        h_b = keep.tile([P, PACK, HALF], F32, name="h_b", tag="gates0")
        nc.sync.dma_start(h_b[:], h_rows[:, :, HALF:J])

        warm = keep.tile([P, 8], F32, name="warm")
        warm2 = keep.tile([P, 8], F32, name="warm2")
        nc.vector.memset(warm[:], 0.0)
        nc.scalar.activation(warm2[:], warm[:], SILU)

        xs = keep.tile([P, S], U8, name="xs", align_bytes=64)
        nc.vector.memset(xs[:].bitcast(I32), 0)
        xs_g = keep.tile([P, S], U8, name="xs_g", align_bytes=64)
        nc.vector.tensor_copy(xs_g[:].rearrange("p (t m) -> p m t", t=PACK), xs_win[:].indirect(offsets[:]))
        for r in range(4):
            eng = nc.scalar if r == 0 else nc.sync
            eng.dma_start(xs[r:P:32, :].bitcast(I32), xs_g[112 + r : P : 4, :].bitcast(I32))
        ew_win = load_words("ew_win", e_words)
        es_g = gather_scales(keep.tile([P, S], U8, name="es_g", align_bytes=64), es_win)
        es = deal_scales(keep.tile([P, S], U8, name="es", align_bytes=64), es_g)
        for r in range(1, 4):
            nc.sync.dma_start(es[4 + r : P : 32, :].bitcast(I32), es[4 + 8 * r : P : 32, :].bitcast(I32))

        h_codes = [keep.tile([P, HALF], U32, name="h_codes0", tag="es_win", align_bytes=64), keep.tile([P, HALF], U32, name="h_codes1", align_bytes=64)]
        h_scales = [keep.tile([P, HALF], U8, name="h_scales%d" % u, align_bytes=64) for u in range(2)]

        def prepare(u, raw):
            hb = keep.tile([P, HALF, PACK], BF16, name="hb%d" % u, align_bytes=64)
            interleave(nc.scalar.copy, hb[:], raw[:])
            quantise(h_codes[u][:], h_scales[u][:], hb[:])

        prepare(0, h_a)
        xw = gather_words(keep.tile([P, PACK, P], U32, name="xw", align_bytes=64), xw_win)
        hb1 = keep.tile([P, HALF, PACK], BF16, name="hb1", align_bytes=64)
        interleave(nc.scalar.copy, hb1[:, 0:144, :], h_b[:, :, 0:144])
        interleave(nc.vector.tensor_copy, hb1[:, 144:HALF, :], h_b[:, :, 144:HALF])
        quantise(h_codes[1][:], h_scales[1][:], hb1[:])
        gates = [keep.tile([P, PACK, HALF], F32, name="gates0", tag="gates0"), keep.tile([P, PACK, HALF], F32, name="gates1")]
        for u in range(2):
            for v in range(2):
                y = passes("y%d%d" % (u, v), xw, xs, 0, (2 * v, 2 * v + 1), h_codes[u][:], h_scales[u][:], HALF)
                nc.scalar.activation(gates[u][:, 2 * v : 2 * v + 2, :], y[:], SILU)
        ew = gather_words(keep.tile([P, PACK, P], U32, name="ew", align_bytes=64), ew_win)

        o_codes = keep.tile([P, J], U32, name="o_codes", align_bytes=64)
        o_scales = keep.tile([P, J], U8, name="o_scales", align_bytes=64)
        o_all = keep.tile([P, PACK, J], F32, name="o_all")
        o = [o_all[:, :, u * HALF : (u + 1) * HALF] for u in range(2)]
        ob = [keep.tile([P, HALF, PACK], BF16, name="ob%d" % u, align_bytes=64) for u in range(2)]
        LO, HI, ALL = slice(0, 128), slice(128, 256), slice(0, 256)

        def values(tag, u, planes, cols):
            bank = psum.tile([P, planes.stop - planes.start, cols.stop - cols.start], F32, name=tag, tag=tag)
            for t in range(planes.start, planes.stop):
                nc.tensor.matmul_mx(out=bank[:, t - planes.start, :], lhsT=ew[:, t, :].bitcast(FP8X4), lhsT_scale=es[4:P, t * P : (t + 1) * P],
                                    rhs=h_codes[u][:, cols].bitcast(FP8X4), rhs_scale=h_scales[u][:, cols], start=True, stop=True)
            return bank

        def multiply(tag, u, planes, cols):
            nc.vector.tensor_tensor(o[u][:, planes, cols], gates[u][:, planes, cols], values(tag, u, planes, cols)[:], MULT)

        def store(u, planes, cols):
            nc.sync.dma_start(out_rows[:, planes, u * HALF + cols.start : u * HALF + cols.stop], o[u][:, planes, cols])

        def round_out(copy, u, cols):
            interleave(copy, ob[u][:, cols, :], o[u][:, :, cols])

        def quantise_out(u, cols):
            at = slice(u * HALF + cols.start, u * HALF + cols.stop)
            nc.vector.quantize_mx(out=o_codes[:, at].bitcast(FP8X4), scales=o_scales[:, at], in_=ob[u][:, cols, :].rearrange("p j t -> p (j t)"))

        def store_words(u):
            at = slice(u * HALF, (u + 1) * HALF)
            nc.sync.dma_start(out_words[:, at], o_codes[:, at].bitcast(I32))

        T0, T1, T2, T01, T23 = slice(0, 1), slice(1, 2), slice(2, 3), slice(0, 2), slice(2, 4)
        multiply("ea", 0, T0, LO)
        multiply("eb", 0, T0, HI)
        store(0, T0, ALL)
        multiply("ec", 0, T1, ALL)
        store(0, T1, ALL)
        e_side = values("ed", 1, T23, LO)
        e_sbuf = keep.tile([P, 2, 128], F32, name="e_sbuf")
        nc.scalar.copy(e_sbuf[:], e_side[:])
        nc.gpsimd.tensor_tensor(o[1][:, T23, LO], e_sbuf[:], gates[1][:, T23, LO], MULT)
        multiply("y00", 0, T23, LO)
        round_out(nc.scalar.copy, 0, LO)
        multiply("y01", 0, T23, HI)
        store(0, T2, ALL)
        round_out(nc.scalar.copy, 0, HI)
        multiply("y10", 1, T23, HI)
        run = slice(2 * J + HALF, PACK * J)
        nc.sync.dma_start(out_0.rearrange("(p t) j -> p (t j)", t=PACK)[:, run], o_all[:].rearrange("p t j -> p (t j)")[:, run])
        multiply("y11", 1, T01, LO)
        multiply("ea", 1, T01, HI)
        store(1, T01, ALL)
        round_out(nc.vector.tensor_copy, 1, LO)
        round_out(nc.scalar.copy, 1, slice(128, 192))
        round_out(nc.vector.tensor_copy, 1, slice(192, 256))
        quantise_out(0, ALL)
        store_words(0)
        quantise_out(1, ALL)
        store_words(1)
        for r in range(4):
            eng = nc.scalar if r % 2 == 0 else nc.sync
            eng.dma_start(out_2[0, r:16:4, :].bitcast(I32), o_scales[r:P:32, :].bitcast(I32))
